import numpy as np, ml_dtypes
CORES = [25,29,65,69,153,157,193,197]
N = 8
BF = ml_dtypes.bfloat16
W, L, C, ST, H = 2048, 256, 8, 6, 1
def parts(rng):
    x = rng.integers(0, 256, (N, 8, 16, W)); z = rng.integers(0, 256, (N, 8, 16, L))
    p = rng.integers(0, W, (N, 8, 16, L)); r = rng.integers(0, W, (N, 8, 16, L))
    return x, p, r, z, rng.integers(1000, 1701, (N, 8))
def pack(x, p, r, z, t):
    return {"xt": np.ascontiguousarray(x.reshape(N, 128, W)).astype(np.float32).astype(BF), "pl": np.ascontiguousarray(p.reshape(N, 128, L)).astype(np.int32),
            "pr": np.ascontiguousarray(r.reshape(N, 128, L)).astype(np.int32), "z0": np.ascontiguousarray(z.reshape(N, 128, L)).astype(np.float32).astype(BF),
            "th": np.repeat(t, 16, axis=1).reshape(N, 128, 1).astype(np.int32)}
def setup_inputs(rng):
    return pack(*parts(rng))
def setup_inputs_spread(rng):
    x, p, r, z, t = parts(rng)
    x = np.floor(256 * np.exp2(-8 * rng.random((N, 8, 1, W))) * rng.random((N, 8, 16, W))); z = np.floor(256 * np.exp2(-8 * rng.random((N, 8, 1, L))) * rng.random((N, 8, 16, L)))
    w = []
    for _ in range(2):
        e = rng.choice(np.array([1.0, 2.0, 4.0]), (N, 8, 1, 1)); n = np.minimum(np.floor(W * rng.random((N, 8, 16, L)) ** e), W - 1).astype(np.int64)
        w.append(np.where(rng.random((N, 8, 1, 1)) < 0.5, n, W - 1 - n))
    t = np.minimum(np.floor(4080 * rng.random((N, 8)) ** 3), 4079)
    return pack(np.minimum(x, 255), w[0], w[1], np.minimum(z, 255), t)
def setup_inputs_ends(rng):
    x, p, r, z, t = parts(rng)
    def bits(n):
        v = 255 * rng.integers(0, 2, (N, 8, 16, n)); c = rng.random((N, 8, 1, n))
        return np.where(c < 0.25, 0, np.where(c > 0.75, 255, v))
    x = bits(W); z = bits(L)
    for g in range(8):
        if g in (0, 3, 7): x[:, g, :, 0] = 0
        elif g in (1, 4): x[:, g, :, 0] = 255
        elif g in (2, 5): x[:, g, :, 0] = 0; x[:, g, 15, 0] = 255
        else: x[:, g, :, 0] = 255 * rng.integers(0, 2, (N, 16))
        x[:, g, :, W - 1] = 255 - x[:, g, :, 0]
    p = np.where(rng.random(p.shape) < 0.8, (W - 1) * rng.integers(0, 2, p.shape), p); r = np.where(rng.random(r.shape) < 0.8, (W - 1) * rng.integers(0, 2, r.shape), r)
    t = 4079 * rng.integers(0, 2, (N, 8)); t[:, 0] = 4079; t[:, 7] = 0
    x[:, 7, :, W - 2] = 0; x[:, 7, 15, W - 2] = 255; z[:, 7, :, L - 1] = 0
    r[:, 7, :15, L - 1] = W - 1; r[:, 7, 15, L - 1] = 0; p[:, 7, :15, L - 1] = W - 1; p[:, 7, 15, L - 1] = W - 2
    z[:, 7, :, L - 2] = 0; r[:, 7, :, L - 2] = W - 1; p[:, 7, 0, L - 2] = 0; p[:, 7, 15, L - 2] = W - 1
    z[:, 1, :, 1] = 255; r[:, 1, :, 1] = W - 1; p[:, 1, 0, 1] = 0; p[:, 1, 15, 1] = W - 1
    return pack(x, p, r, z, t)
def setup_inputs_crowd(rng):
    x, p, r, z, t = parts(rng); x[..., 0] = 0; x[..., W - 1] = 255
    q = rng.integers(0, 16, (N, 8, 1, L)); m = (np.arange(16).reshape(1, 1, 16, 1) - q) & 15; lane = np.arange(L)
    b = rng.integers(0, 2, (N, 8, 1, L)); z = np.broadcast_to(255 * b, (N, 8, 16, L))
    far = np.where(rng.random(r.shape) < 0.5, (W - 1) * (1 - b), rng.integers(1, W - 1, r.shape))
    r = np.where(m == 0, (W - 1) * b, far)
    own = (W - 1) * rng.integers(0, 2, (N, 8, 1, L)); e = (m >= 1) & (m < 8)
    e[:, 1::2, :, L - 1] &= m[:, 1::2, :, L - 1] != 7
    e[:, 2] &= (m[:, 2] == 1) & (lane < 32); e[:, 3] &= (m[:, 3] == 1) & (lane < 31); e[:, 6] = False
    p = np.where(e, W - 1 - own, np.where(m < 8, own, p))
    return pack(x, p, r, z, rng.choice(np.array([0, 1000, 1400, 4079]), (N, 8)))
def setup_inputs_ties(rng):
    x, p, r, z, t = parts(rng)
    x = rng.integers(0, 4, x.shape); z = rng.integers(0, 4, z.shape); x[:, 1] += 252; x[:, 6] += 252; z[:, 6] += 252
    same = rng.random((N, 8, 1, L)) < 0.25
    p = np.where(same, np.roll(np.repeat(p[:, :, :4], 4, axis=2), 1, axis=2), p); r = np.where(same, np.tile(r[:, :, :4], (1, 1, 4, 1)), r)
    t = rng.integers(0, 19, (N, 8)); t[:, 3] = 0; near = np.array([3, 5, 7, 9, 19, 21])
    p[:, 3] = W - rng.choice(near, (N, 16, L)); r[:, 3] = W - rng.choice(near, (N, 16, L))
    return pack(x, p, r, z, t)
def setup_inputs_corners(rng):
    x, p, r, z, t = parts(rng); i = np.arange(L).reshape(1, 1, L); j = np.arange(16).reshape(1, 16, 1)
    p[:, 0] = rng.integers(0, W, (N, 16, 1)); r[:, 0] = rng.integers(0, W, (N, 16, 1))
    p[:, 1] = rng.integers(0, W, (N, 1, L)); r[:, 1] = rng.integers(0, W, (N, 1, L))
    p[:, 2] = C * i + (j & (C - 1)); r[:, 2] = C * i + (C - 1 - (j & (C - 1)))
    p[:, 3] = r[:, 3]
    p[:, 4] = ((W - 1) * (np.arange(N) & 1)).reshape(N, 1, 1); r[:, 4] = W - 1 - p[:, 4]
    o = np.argsort(rng.random((N, max(W, 16 * L))), axis=1)[:, :16 * L] & (W - 1)
    p[:, 5] = o.reshape(N, 16, L); r[:, 5] = W - 1 - p[:, 5, ::-1]
    p[:, 6] = C * ((i + 1) % L) + ((j + rng.integers(0, C, (N, 1, 1))) & (C - 1)); r[:, 6] = C * ((i + L - 1) % L) + ((j + rng.integers(0, C, (N, 1, 1))) & (C - 1))
    p[:, 7, :, :L - 1] = ((W - 1) * ((i + j) & 1))[:, :, :L - 1]; r[:, 7, :, :L - 1] = (W - 1) * (j & 1)
    t = rng.choice(np.array([0, 500, 1200, 2000, 4079]), (N, 8)); t[:, 5] = 2048
    z[:, 5] = 255 * rng.integers(0, 2, (N, 1, L)); z[:, 5, :, L - 1] = 0
    x[:, 5, :, 0] = 0; x[:, 5, :, W - 1] = 0; x[:, 5, :8, W - 1] = 255; x[:, 5, 8, W - 1] = 9
    r[:, 5, :8, L - 1] = W - 1; r[:, 5, 15, L - 1] = 0; p[:, 5, :7, L - 1] = W - 1; p[:, 5, 15, L - 1] = 0
    return pack(x, p, r, z, t)
def check_inputs(d):
    bad = []
    for k, lo, hi in (("xt", 0, 255), ("pl", 0, W - 1), ("pr", 0, W - 1), ("z0", 0, 255), ("th", 0, 4079)):
        a = np.asarray(d[k]).astype(np.float64)
        if not (np.min(a) >= lo and np.max(a) <= hi): bad.append("range of " + k)
        if np.any(a != np.floor(a)): bad.append("whole numbers in " + k)
    a = np.asarray(d["th"]).reshape(-1, 16)
    if np.any(a != a[:, :1]): bad.append("the 16 rows of a group in th are alike")
    return bad
def turn(q, s):
    return np.take_along_axis(q, (np.arange(16).reshape(1, 1, 16, 1) + s[:, :, None, :]) & 15, 2)
def items(x, n):
    return np.take_along_axis(x, n.reshape(N, 8, 1, 16 * L), 3).reshape(N, 8, 16, 16, L)
def reference(xt, pl, pr, z0, th):
    x = xt.astype(np.float32).astype(np.int64).reshape(N, 8, 16, W); z = z0.astype(np.float32).astype(np.int64).reshape(N, 8, 16, L)
    p = pl.astype(np.int64).reshape(N, 8, 16, L); r = pr.astype(np.int64).reshape(N, 8, 16, L)
    t = th.astype(np.int64).reshape(N, 8, 16)[:, :, 0]; a = np.zeros((N, 8), np.int64)
    for step in range(ST):
        d = np.add.reduce(np.abs(items(x, r) - z[:, :, :, None, :]), axis=2)
        k = np.argmin(d, axis=2)
        v = items(x, p); y = np.take_along_axis(v, k[:, :, None, None, :], 3)[:, :, :, 0, :]
        f = np.add.reduce(np.abs(v - y[:, :, :, None, :]), axis=2)
        p = turn(p, k); f = turn(f, k); r = turn(r, k + 1); d = turn(d, k + 1)
        lim = (t + (a & 31))[:, :, None, None]; left = f[:, :, 1:8] > lim; right = d[:, :, 1:8] > lim
        p1, p9, r1, r9 = p[:, :, 1:8], p[:, :, 9:16], r[:, :, 1:8], r[:, :, 9:16]
        new = ((p1 * r1 >> 5) + p1 + a[:, :, None, None]) & (W - 1)
        p = np.concatenate([p[:, :, :1], np.where(left, p9, p1), p[:, :, 8:9], np.where(left, new, p9)], axis=2)
        r = np.concatenate([r[:, :, :1], np.where(right, r9, r1), r[:, :, 8:9], np.where(right, r1, r9)], axis=2)
        u = np.add.reduce(y, axis=2)
        np.put_along_axis(x, (C * np.arange(L) + (u & (C - 1)))[:, :, None, :], (y + z) >> 1, 3)
        z = np.abs(y - z)
        if step < ST - 1:
            a = np.add.reduce(left.astype(np.int64), axis=(2, 3))
            p = np.roll(p, H, axis=0); r = np.roll(r, H, axis=0); z = np.roll(z, H, axis=0)
    return {"yx": x.reshape(N, 128, W).astype(np.float32).astype(BF), "yp": p.reshape(N, 128, L).astype(np.float32),
            "yr": r.reshape(N, 128, L).astype(np.float32), "yz": z.reshape(N, 128, L).astype(np.float32).astype(BF)}

@@ -1,0 +1,703 @@
+import numpy as np
+from concourse.mybir import AluOpType as Op, ActivationFunctionType as Act
+
+ST = 6
+BIG = float(2 ** 27)
+MAGIC = float(3 * 2 ** 22)
+F, H, I, U = "float32", "bfloat16", "int32", "uint16"
+
+
+def _sb(n, d):
+    return ("sbuf", [128, n], d)
+
+
+SCRATCH = {
+    "tab": _sb(2048, H), "tab2": _sb(2048, H), "vv": _sb(2048, H), "dd": _sb(2048, H), "ab": _sb(4096, H),
+    "vp": _sb(2048, H), "dp": _sb(2048, H), "abp": _sb(2048, H), "t2": _sb(128, F),
+    "zz": _sb(256 * ST, H), "zo": _sb(256 * ST, H), "jw": _sb(256 * ST, H), "jo": _sb(256 * ST, H),
+    "pp": _sb(256 * ST, F), "po": _sb(256 * ST, F),
+    "ru": _sb(256 * ST, U), "rs": _sb(256 * ST, F), "idf": _sb(128, F), "idh": _sb(128, H), "qtr": _sb(256, H), "wn2": _sb(144, H), "wp1": _sb(144, H), "wm1": _sb(144, H),
+    "pin": _sb(256, I), "rin": _sb(256, I), "thi": _sb(4, I), "ta": _sb(256, F), "tb": _sb(256, F), "tc": _sb(512, F),
+    "td": _sb(256, F), "te": _sb(256, F), "ti": _sb(256, I), "tj": _sb(256, I), "op": _sb(256, F), "orr": _sb(256, F),
+    "col": _sb(16, F), "coli": _sb(8, I), "cidx": _sb(144, F), "blk": _sb(128, F), "blki": _sb(128, F),
+    "wneg": _sb(144, H), "wpos": _sb(144, H), "idp": _sb(128, H), "idn": _sb(128, H), "cst": _sb(384, H),
+    "li": _sb(160, I), "lh": _sb(48, I), "lr": _sb(48, I), "lu": _sb(160, U), "base": _sb(16, I), "q2": _sb(128, I),
+    "khs": _sb(128, F), "m1": _sb(256, F), "x0": _sb(128, I), "x1": _sb(128, I), "sp": _sb(128, I), "sr": _sb(128, I),
+    "jp": _sb(128, I), "pf": _sb(128, F), "m2": _sb(256, F), "yu": _sb(16, U), "pu": _sb(128, U),
+    "yy": _sb(256, H), "dz": _sb(256, H), "hm": _sb(256, F), "avg": _sb(256, H),
+    "ui": _sb(48, I), "uu": _sb(16, U), "thr": _sb(128, F), "tq": _sb(128, F), "wn": _sb(128, F), "rf": _sb(128, F),
+    "prod": _sb(128, F), "pa": _sb(128, I), "new": _sb(128, I), "dlo": _sb(128, F), "dhi": _sb(128, F), "ahi": _sb(128, F),
+    "sg": _sb(128, F), "cnt": _sb(4, F), "ai": _sb(8, I), "lim": _sb(16, F), "bits": _sb(512, I),
+    "s0": ("psum", [128, 512], F), "s1": ("psum", [128, 512], F), "s2": ("psum", [128, 512], F), "s3": ("psum", [128, 512], F),
+    "klo": ("psum", [128, 512], F), "khi": ("psum", [128, 512], F), "msc": ("psum", [128, 512], F), "vt": ("psum", [128, 512], F),
+}
+STREAMS = {"ru": ("ru", 0, 256), "ra": ("rs", 0, 128), "rb": ("rs", 128, 256), "zz": ("zz", 0, 256), "jw": ("jw", 0, 256),
+           "pa": ("pp", 0, 128), "pb": ("pp", 128, 256)}
+CFG = {"npa": 6, "npa_last": 6, "nrelu": 4, "khs": "a", "early": 2, "fill": 4, "y": "v", "avg": "v", "db": 0, "inorder": "", "phase": 1, "prelu": 0, "ford": (0, 1)}
+PAR = {"c": 1.0, "g": 1.5, "scat": 3.8, "fix": 30.0, "pe": 0.5, "wake": 100.0, "issue": 400.0, "hop": 4500.0, "w": 2 / 120}
+PARS = [PAR, dict(PAR, g=1.04, scat=1.6, wake=50.0, hop=3000.0, w=1 / 100), dict(PAR, g=2.08, scat=6.0, wake=200.0, pe=0.83, hop=5500.0, w=1 / 160),
+        dict(PAR, hop=2500.0, fix=60.0, pe=0.42, wake=150.0, w=1 / 120)]
+TRIES = [3000, 1, 1.0]
+MOVED = {x.split(":")[0]: 100 * int(x.split(":")[1]) for x in (
+    "aab2:-1 aab6:-10 aabp1:5 aabp2:21 aabp3:-5 aabp4:19 ajo1:6 asg1:-10 avp1:-8 avp3:44 avv1:6 avv3:-8 avv4:-7 avv5:-4 awn21:42 "
+    "azo1:3 gjo1:-10 gli2:34 gpo1:2 gq21:75 gzo1:9 laab5:-1 laabp3:-3 lakhi1:-2 lasg1:-10 ltkhi5:-10 ltkhi6:-10 ltkhi7:-10 ltklo6:-2 "
+    "ltklo7:-9 lts05:-10 lts16:-10 lts34:6 lts35:3 lvahi1:-4 lvdd1:-2 lvdd2:19 lvdhi1:3 lvdlo1:13 lvm21:-10 lvm23:-10 lvnew1:-10 "
+    "lvpo2:-1 lvprod1:20 lvrf1:2 lvsr1:-10 lvt21:-10 lvtq1:-10 lvvt1:-5 lvvt3:65 lvvt4:5 lvvt5:-6 lvx01:-4 lvx11:2 lvyy1:1 tkhi2:26 "
+    "tklo5:5 tklo6:-5 tklo7:1 tmsc1:22 tmsc2:67 ts01:-10 ts03:10 ts06:12 ts15:24 ts21:3 vab2:-7 vahi1:-2 vavg1:5 vcol52:28 vcoli2:57 "
+    "vdhi1:-10 vdp1:73 vdp2:80 vkhs1:7 vm12:-9 vm13:-3 vm14:-7 vm21:100 vpo2:-10 vpp1:16 vpu1:66 vsp1:-8 vt21:4 vt251:-1 vuu1:38 "
+    "vvt2:27 vvt5:19 vvt6:49 vvt7:-9 vx01:-10 vx11:31").split()}
+PLAN = {}
+ORDER = [("ru", 1)] + [x for t in range(1, ST) for x in (
+    ("ru", t + 1), ("ra", t), ("rb", t), ("zz", t), ("jw", t), ("pa", t), ("pb", t)) if x[1] < ST]
+
+
+def relay_of(s, t):
+    return {"ru": 2 * (1 - t % 2), "zz": 0, "ra": 3, "rb": 1, "jw": 3, "pa": 2, "pb": 1}[s]
+
+
+SEMAPHORES = (["cv", "ca", "ct", "cg", "ldr", "ldx", "ldz", "ldp", "sto", "sent", "cpy"]
+              + ["a%s%d" % (s, t) for s in STREAMS for t in range(1, ST)])
+
+
+def relays(T, topo, rank):
+    src, dst = T.cores[rank], T.cores[(rank + 1) % len(T.cores)]
+    if topo.may_write(src, dst):
+        return []
+    c = [x for x in topo.cores_of(src) if T.rank_of(x) is None and topo.may_write(x, dst)]
+    return sorted(c, key=lambda x: topo.die(x) != topo.die(src))
+
+
+def slot(T, s, t):
+    name, a, b = STREAMS[s]
+    return T[name][:, 256 * t + a:256 * t + b]
+
+
+def relay_program(g, core, T, topo):
+    n = len(T.cores)
+    for r in range(n):
+        rl = relays(T, topo, r)
+        if core not in rl:
+            continue
+        src, dst = T.cores[r], T.cores[(r + 1) % n]
+        got, m = len(topo.engines(src, core)), topo.mask(core, dst)
+        rid, pid = topo.addr(dst, core)
+        sent = 0
+        for s, t in ORDER:
+            if rl[relay_of(s, t)] == core:
+                sem = T.sem["a%s%d" % (s, t)]
+                g.wait_ge(sem, got)
+                g.remote_dma(slot(T, s, t), slot(T, s, t), sem, T.sem.sent, pid, rid, m)
+                sent += len(topo.engines(core, dst))
+        g.wait_ge(T.sem.sent, sent)
+
+
+def rank_program(g, core, T, topo):
+    rank = T.rank_of(core)
+    if rank is None:
+        return relay_program(g, core, T, topo)
+    n = len(T.cores)
+    nxt, prv = T.cores[(rank + 1) % n], T.cores[(rank - 1) % n]
+    rl_out, rl_in = relays(T, topo, rank), relays(T, topo, (rank - 1) % n)
+
+    Q = {"v": g.vector, "a": g.scalar, "t": g.tensor, "g": g, "s": g.sync}
+    SEM = {"v": "cv", "a": "ca", "t": "ct", "g": "cg"}
+    cnt = {"cv": 0, "ca": 0, "ct": 0, "cg": 0, "sent": 0, "sto": 0, "cpy": 0}
+    known = {q: {} for q in Q}
+    hist = {}
+    psum = [k for k in SCRATCH if SCRATCH[k][0] == "psum"]
+
+    def V(name, a=0, b=None, step=1):
+        return (name, a, SCRATCH[name][1][1] if b is None else b, step)
+
+    def G(win, off):
+        return ("ind", win, off)
+
+    def ap(v):
+        if v[0] == "ind":
+            return ap(v[1]).indirect(ap(v[2]))
+        return T[v[0]][:, v[1]:v[2]] if v[3] == 1 else T[v[0]][:, v[1]:v[2]:v[3]]
+
+    def arg(v):
+        return ap(v) if isinstance(v, tuple) else v
+
+    ops, sends, banks, seen = [], {}, {}, {}
+
+    def size(v):
+        return 16 * (v[2][2] - v[2][1]) if v[0] == "ind" else len(range(v[1], v[2], v[3]))
+
+    def cost(q, outs, ins, PAR):
+        o, m = outs[0], size(outs[0])
+        vs = [v for v in ins if isinstance(v, tuple)]
+        if q == "t":
+            return max(64, m) * PAR["pe"] * (4 if SCRATCH[vs[0][0]][2] == F else 1)
+        if q == "g":
+            return 130 + 2 * m * PAR["c"]
+        if o[0] == "ind":
+            return 50 + m * PAR["scat"] * PAR["c"]
+        if any(v[0] == "ind" for v in vs):
+            return 55 + m * PAR["g"] * PAR["c"]
+        full = [v for v in vs if size(v) == m]
+        per = 1.0
+        if q == "v" and len(full) == 2 and not any(v[0] in psum for v in full):
+            per = 2.0
+        elif q == "v" and all(SCRATCH[v[0]][2] in (H, U) for v in full + [o]):
+            per = 0.5
+        return PAR["fix"] + max(64, m * per) * PAR["c"]
+
+    def split(outs, ins):
+        wr, rd = [], []
+        for v in outs:
+            if v[0] == "ind":
+                wr.append(v[1]); rd.append(v[2])
+            else:
+                wr.append(v)
+        for v in ins:
+            if isinstance(v, tuple):
+                if v[0] == "ind":
+                    rd.append(v[1]); rd.append(v[2])
+                else:
+                    rd.append(v)
+        return wr, rd
+
+    def record(q, wr, rd, call, c, kind="c", order=(), lat=None, tok=None):
+        wait, order, me = set(), set(order), len(ops)
+        for kd, vs in (("w", wr), ("r", rd)):
+            for v in vs:
+                for (a, b, k2, q2, i) in hist.get(v[0], []):
+                    if v[3] == 2 and v[1] == a + 1 and k2 == "w" and i == me - 1:
+                        continue
+                    if not (q == "t" and q2 == "t") and a < v[2] and v[1] < b and (kd == "w" or k2 == "w"):
+                        (order if kd == "w" and q == q2 and q in CFG["inorder"] else wait).add(i)
+        for name in set(v[0] for v in wr + rd if v[0] in psum):
+            bk = banks.setdefault(name, {"q": q, "now": [], "was": [], "pe": []})
+            if bk["q"] != q:
+                bk.update(q=q, was=bk["now"], now=[])
+            wait.update(bk["was"])
+            bk["now"].append(me)
+            if q == "t":
+                order.update(bk["pe"])
+                bk["pe"] = [me]
+        name = q + (wr[0][0] if wr else rd[0][0])
+        seen[name] = seen.get(name, 0) + 1
+        ops.append({"id": "%s%s%d" % (seen.get("phase", ""), name, seen[name]), "q": q, "call": call, "cs": [c(p) for p in PARS],
+                    "ls": [lat(p) for p in PARS] if lat else [0.0] * len(PARS), "c": c(PAR), "lat": lat(PAR) if lat else 0.0,
+                    "kind": kind, "wait": sorted(wait), "order": sorted(order), "tok": tok})
+        for v in wr:
+            hist[v[0]] = [e for e in hist.get(v[0], []) if not (v[1] <= e[0] and e[1] <= v[2])] + [(v[1], v[2], "w", q, me)]
+        for v in rd if kind in "cm" else []:
+            hist[v[0]] = hist.get(v[0], []) + [(v[1], v[2], "r", q, me)]
+        return me
+
+    def run(q, outs, ins, call):
+        wr, rd = split(outs, ins)
+        record(q, wr, rd, call, lambda p: cost(q, outs, ins, p))
+
+    def length(order):
+        total = []
+        for k, p in enumerate(PARS):
+            free, fin = {}, [0.0] * len(ops)
+            for i in order:
+                o = ops[i]
+                t0 = free.get(o["q"], 0.0)
+                for j in o["wait"]:
+                    if fin[j] + p["wake"] > t0:
+                        t0 = fin[j] + p["wake"]
+                if o["q"] == "x":
+                    t0 = max([t0] + [fin[j] for j in o["order"]])
+                else:
+                    free[o["q"]] = t0 + o["cs"][k]
+                fin[i] = t0 + o["cs"][k] + o["ls"][k]
+            total.append(max(fin))
+        return sum(x * p["w"] for x, p in zip(total, PARS)), total
+
+    def best_plan():
+        rng = np.random.RandomState(TRIES[1])
+        ids = sorted(o["id"] for o in ops if o["q"] in "vatg")
+        boost = dict(MOVED)
+        order = plan(boost)
+        best = now = length(order)
+        kept = boost
+        for it in range(TRIES[0]):
+            b = dict(boost)
+            for _ in range(1 + int(rng.randint(3))):
+                k = ids[rng.randint(len(ids))]
+                u = rng.rand()
+                b[k] = 0 if u < 0.2 else max(-1000, b.get(k, 0) + 100 * int(rng.randn() * (4 if u < 0.6 else 20)))
+            od = plan(b)
+            x = length(od)
+            if x[0] <= now[0] + TRIES[2] * (1.0 - it / TRIES[0]) * rng.exponential():
+                boost, now = b, x
+                if x[0] <= best[0]:
+                    kept, order, best = b, od, x
+        PLAN.update(length=best, kept=kept, plan=plan, weigh=length)
+        return order
+
+    def plan(boost):
+        m = len(ops)
+        up = [0.0] * m
+        for i in range(m - 1, -1, -1):
+            up[i] += max(1.0, ops[i]["c"] + boost.get(ops[i]["id"], 0)) + ops[i]["lat"]
+            for j in ops[i]["wait"]:
+                up[j] = max(up[j], up[i] + PAR["wake"])
+            for j in ops[i]["order"]:
+                up[j] = max(up[j], up[i] - (0.0 if ops[i]["q"] == "x" else ops[j]["lat"]))
+        start, busy = [0.0] * m, {q: [] for q in Q}
+        for i in sorted(range(m), key=lambda i: (-up[i], i)):
+            o = ops[i]
+            t0 = max([start[j] + ops[j]["c"] + ops[j]["lat"] + PAR["wake"] for j in o["wait"]]
+                     + [start[j] + ops[j]["c"] + (ops[j]["lat"] if o["q"] == "x" else 0.001) for j in o["order"]] + [0.0])
+            if o["q"] != "x":
+                b = busy[o["q"]]
+                k = bisect(b, t0)
+                while k < len(b) and b[k][0] < t0 + o["c"]:
+                    t0 = max(t0, b[k][1])
+                    k += 1
+                b.insert(k, (t0, t0 + o["c"]))
+            start[i] = t0
+        return sorted(range(m), key=lambda i: (start[i], i))
+
+    def bisect(b, t0):
+        lo, hi = 0, len(b)
+        while lo < hi:
+            mid = (lo + hi) // 2
+            if b[mid][1] <= t0:
+                lo = mid + 1
+            else:
+                hi = mid
+        return lo
+
+    def emit():
+        if "order" not in PLAN:
+            PLAN["order"] = best_plan()
+        for i in PLAN["order"]:
+            o = ops[i]
+            q = o["q"]
+            if q == "x":
+                continue
+            toks, k = {}, known[q]
+            for j in o["wait"]:
+                tk = ops[j]["tok"]
+                if tk[0] not in toks or toks[tk[0]][1] < tk[1]:
+                    toks[tk[0]] = tk
+            for sem, val, clock in sorted(toks.values(), key=lambda tk: tk[0] == SEM.get(q)):
+                if k.get(sem, 0) < val:
+                    Q[q].wait_ge(T.sem[sem], val)
+                    k[sem] = val
+                    for s in clock:
+                        k[s] = max(k.get(s, 0), clock[s])
+            if o["kind"] == "c":
+                cnt[SEM[q]] += 1
+                o["call"]().then_inc(T.sem[SEM[q]], 1)
+                o["tok"] = (SEM[q], cnt[SEM[q]], dict(k))
+            elif o["kind"] == "m":
+                cnt["cpy"] += 16
+                o["call"]().then_inc(T.sem.cpy, 16)
+                o["tok"] = ("cpy", cnt["cpy"], dict(k))
+            else:
+                o["call"]()
+
+    def tt(o, a, b, op):
+        run("v", [o], [a, b], lambda: g.vector.tensor_tensor(ap(o), ap(a), ap(b), op))
+
+    def ts(o, a, s1, op0, s2=None, op1=None):
+        if op1 is None:
+            run("v", [o], [a, s1], lambda: g.vector.tensor_scalar(ap(o), ap(a), arg(s1), None, op0))
+        else:
+            run("v", [o], [a, s1, s2], lambda: g.vector.tensor_scalar(ap(o), ap(a), arg(s1), arg(s2), op0, op1))
+
+    def cp(o, a):
+        run("v", [o], [a], lambda: g.vector.tensor_copy(ap(o), ap(a)))
+
+    def ms(o, c):
+        run("v", [o], [], lambda: g.vector.memset(ap(o), c))
+
+    def tr(o, a):
+        run("v", [o], [a], lambda: g.vector.transpose(ap(o), ap(a)))
+
+    def act(o, a, f, bias=0.0, scale=1.0, acc=None):
+        if acc is None:
+            run("a", [o], [a, bias, scale], lambda: g.scalar.activation(ap(o), ap(a), f, bias=arg(bias), scale=arg(scale)))
+        else:
+            run("a", [o, acc], [a, bias, scale],
+                lambda: g.scalar.activation(ap(o), ap(a), f, bias=arg(bias), scale=arg(scale), accum_out=ap(acc)))
+
+    def mm(o, w, x, start, stop):
+        run("t", [o], [w, x], lambda: g.tensor.matmul(ap(o), ap(w), ap(x), start, stop))
+
+    def iota(o, pat, base=0, cm=0):
+        if SCRATCH[o[0]][2] == I:
+            run("g", [o], [], lambda: g.iota(ap(o), pat, base, cm))
+        else:
+            run("g", [o], [], lambda: g.iota(ap(o), pat, base, cm, allow_small_or_imprecise_dtypes=True))
+
+    def landed(v, sem, val, at, order=()):
+        record("x", [v], [], None, lambda p: 0.0, "x", order, lambda p: at, (sem, val, {}))
+
+    def send(s, src, t, after=()):
+        to = rl_out[relay_of(s, t)] if rl_out else nxt
+        rid, pid = topo.addr(to, core)
+        cnt["sent"] += len(topo.engines(core, to))
+        me = record("g", [], [src] + list(after), lambda: g.remote_dma(
+            slot(T, s, t), ap(src), T.sem["a%s%d" % (s, t)], T.sem.sent, pid, rid, topo.mask(core, to)),
+            lambda p: p["issue"], "r", [sends["last"]] if sends else [], lambda p: p["hop"])
+        assert ORDER[sends.get("n", 0)] == (s, t)
+        sends.update(last=me, n=sends.get("n", 0) + 1)
+        landed(S(STREAMS[s][0], t, STREAMS[s][1], STREAMS[s][2]), "a%s%d" % (s, t), len(topo.engines(rl_in[relay_of(s, t)] if rl_in else prv, core)), 0.0, [me])
+
+    def store(q, dst, src, v, lat=2200.0):
+        cnt["sto"] += 16
+        record(q, [], [v], lambda: Q[q].dma_start(dst, src).then_inc(T.sem.sto, 16), lambda p: 100.0, "d", (), lambda p: lat)
+
+    def blocks():
+        for gg in range(4):
+            for x in range(2):
+                for y in range(2):
+                    yield (slice(32 * gg + 16 * x, 32 * gg + 16 * x + 16), slice(128 * y, 128 * y + 128),
+                           slice(32 * gg + 16 * y, 32 * gg + 16 * y + 16), slice(128 * x, 128 * x + 128))
+
+    def S(name, t, a=0, b=None):
+        return V(name, 256 * t + a, 256 * t + (256 if b is None else b))
+
+    for k, (sp_, sc_, dp_, dc_) in enumerate(blocks()):
+        Q["sa"[k % 2]].dma_start(T.rin[sp_, sc_], T.pr[dp_, dc_]).then_inc(T.sem.ldr, 16)
+    g.sync.dma_start(T.tab[:], T.xt[:]).then_inc(T.sem.ldx, 16)
+    g.scalar.dma_start(T.zz[:, 0:256], T.z0[:]).then_inc(T.sem.ldz, 16)
+    g.scalar.dma_start(T.thi[:, 0:1], T.th[:], ).then_inc(T.sem.ldz, 16)
+    for (sp_, sc_, dp_, dc_) in blocks():
+        g.sync.dma_start(T.pin[sp_, sc_], T.pl[dp_, dc_]).then_inc(T.sem.ldp, 16)
+    landed(V("rin"), "ldr", 256, 2500.0); landed(V("tab"), "ldx", 16, 4500.0); landed(S("zz", 0), "ldz", 32, 3000.0)
+    landed(V("thi"), "ldz", 32, 3000.0); landed(V("pin"), "ldp", 256, 4500.0)
+
+    def C(k):
+        return V("col", k, k + 1)
+    P1, BC, INV2, SH1, PK, B1, B2, B3, P2, INV1 = [V("lu", a, b) for a, b in (
+        (0, 16), (16, 24), (24, 40), (40, 48), (48, 64), (64, 72), (72, 80), (80, 88), (120, 136), (136, 152))]
+
+    def TAB(t):
+        return V("tab2" if CFG["db"] and t % 2 else "tab")
+    iota(V("coli", 0, 1), [[0, 1]], 0, 1)
+    iota(V("li", 0, 16), [[16, 8], [128, 2]])
+    iota(V("li", 120, 136), [[1, 16]])
+    iota(V("cidx"), [[1, 144]])
+    iota(V("q2"), [[2048, 8], [0, 16]])
+    iota(V("li", 16, 24), [[0, 8]])
+    iota(V("li", 24, 40), [[16, 2], [32, 8]])
+    iota(V("lr", 0, 8), [[16, 8]], 16)
+    iota(V("lr", 8, 24), [[16, 8], [0, 2]], 16)
+    iota(V("lh", 0, 8), [[0, 8]])
+    iota(V("lh", 8, 24), [[0, 8], [128, 2]])
+    iota(V("li", 64, 72), [[16, 4], [0, 2]])
+    iota(V("li", 72, 80), [[16, 2], [0, 2], [8, 2]])
+    iota(V("li", 80, 88), [[0, 2], [4, 4]])
+    iota(V("li", 136, 152), [[8, 8], [64, 2]])
+    iota(V("base"), [[128, 16]])
+    iota(V("blki"), [[16, 8], [0, 16]])
+
+    ts(V("coli", 1, 2), V("coli", 0, 1), 15, Op.bitwise_and)
+    ts(V("coli", 2, 3), V("coli", 0, 1), 7, Op.bitwise_and)
+    ts(V("coli", 3, 4), V("coli", 0, 1), 8, Op.bitwise_and)
+    cp(C(0), V("coli", 1, 2))
+    ts(C(1), V("coli", 2, 3), 32.0, Op.mult)
+    ts(P1, V("li", 0, 16), C(0), Op.add)
+    ts(C(2), V("coli", 3, 4), 2.0, Op.mult, C(1), Op.add)
+    cp(C(3), V("coli", 0, 1))
+    ts(P2, V("li", 120, 136), C(2), Op.add)
+    ts(C(4), C(3), C(0), Op.subtract)
+    ts(V("idp"), V("cidx", 0, 128), C(3), Op.is_equal)
+    ts(C(5), C(4), 15.0, Op.add)
+    ts(V("idn"), V("cidx", 0, 128), C(3), Op.is_equal, -1.0, Op.mult)
+    ts(V("wneg"), V("cidx"), C(5), Op.is_equal, -32768.0, Op.mult)
+    cp(V("ta"), G(V("rin"), P1))
+    ms(V("cst", 0, 128), BIG)
+    tr(V("tb"), V("ta"))
+    ms(V("cst", 128, 256), -2048.0)
+    cp(S("ru", 0), G(V("tb"), P2))
+    send("ru", S("ru", 0), 1)
+    ms(V("cst", 256, 384), -14336.0)
+    act(V("wn2"), V("wneg"), Act.Identity, 0.0, 2.0)
+    act(V("wp1"), V("wneg"), Act.Identity, 0.0, -1.0)
+    act(V("wpos"), V("wneg"), Act.Identity, 0.0, -2.0 ** -15)
+    act(V("wm1"), V("wneg"), Act.Identity, 0.0, 2.0 ** -15)
+    act(V("idf"), V("idp"), Act.Copy)
+    act(V("idh"), V("idp"), Act.Identity, 0.0, 0.5)
+    ms(V("qtr"), -0.5)
+
+    def LIM(k):
+        return V("lim", k, k + 1)
+
+    def sums(bank, o, src, rows, w, start, stop, buf="ab"):
+        out = V(bank, o, o + 16 * rows)
+
+        def call():
+            for a in range(16):
+                last = g.tensor.matmul(ap(out), ap(V(w, 15 - a, 143 - a)), ap(V(buf, src + a, src + 256 * rows, 16)),
+                                       start and a == 0, stop and a == 15)
+            return last
+        record("t", [out], [V(w), V(buf, src, src + 256 * rows)], call, lambda p: 16 * max(64, 16 * rows) * p["pe"])
+
+    def pregather(t, k, into=True):
+        q = (2 * k + t) % 8
+        if q == 7:
+            act(V("vv", 512 * k, 512 * k + 256), G(TAB(t), S("ru", t, 240, 256)), Act.Copy)
+            act(V("vv", 512 * k + 256, 512 * k + 512), G(TAB(t), S("ru", t, 128, 144)), Act.Copy)
+        else:
+            act(V("vv", 512 * k, 512 * k + 512), G(TAB(t), S("ru", t, 128 + 16 * q, 160 + 16 * q)), Act.Copy)
+        if into:
+            mm(V("s%d" % k), V("idp"), V("vv", 512 * k, 512 * k + 512), True, False)
+
+    def turned(o, t, half):
+        c = 128 - 16 * t
+        mm(V("s2", o, o + c), V("idf"), S("rs", t, half + 16 * t, half + 128), True, True)
+        if t:
+            mm(V("s2", o + c, o + 128), V("idf"), S("rs", t, half, half + 16 * t), True, True)
+
+    def limits():
+        ts(LIM(0), V("ai", 1, 2), -32768.0, Op.mult, LIM(4), Op.add)
+        ts(LIM(1), V("ai", 1, 2), -1.0, Op.mult, LIM(5), Op.add)
+
+    for k in range(4):
+        pregather(0, k, k == 0)
+
+    def VT(k):
+        return V("vt", 128 * k, 128 * k + 128)
+
+    def setup_rest():
+        yield lambda: cp(V("tc", 0, 256), S("ru", 0))
+        yield lambda: cp(V("td"), G(V("pin"), P1))
+        yield lambda: (tt(S("rs", 0, 128, 256), V("tc", 128, 256), V("tc", 0, 128), Op.subtract),
+                       ts(S("rs", 0, 0, 128), V("tc", 0, 128), 32.0, Op.add))
+        yield lambda: (tr(V("te"), V("td")), cp(S("jw", 0, 0, 128), V("q2")))
+        yield lambda: (ms(S("jw", 0, 128, 256), -2048.0), ts(V("lr", 0, 24), V("lr", 0, 24), 127, Op.bitwise_and))
+        yield lambda: (cp(S("pp", 0), G(V("te"), P2)), tt(V("li", 40, 64), V("lr", 0, 24), V("lh", 0, 24), Op.add), act(C(6), C(0), Act.Identity, 0.0, 8.0))
+        yield lambda: (cp(LIM(3), V("thi", 0, 1)), ms(LIM(2), 0.0), ts(V("lu", 16, 72), V("li", 16, 72), C(0), Op.add),
+                       ts(V("base"), V("base"), C(6), Op.add),
+                       act(LIM(4), LIM(3), Act.Identity, BIG - 31744.0, -32768.0), act(LIM(5), LIM(3), Act.Identity, -0.5, -1.0),
+                       act(LIM(0), LIM(4), Act.Copy), act(LIM(1), LIM(5), Act.Copy))
+        yield lambda: ts(V("blk"), V("blki"), C(4), Op.is_equal)
+
+    for t in range(ST):
+        last = t == ST - 1
+        seen.clear()
+        seen["phase"] = "l" if last and CFG["phase"] else ""
+        z, J, Wm = S("zz", t), S("jw", t, 0, 128), S("jw", t, 128, 256)
+        plo, phi = S("pp", t, 0, 128), S("pp", t, 128, 256)
+        WmP, rlo, dR = V("s2", 0, 128), V("s2", 128, 256), V("s2", 256, 384)
+        KL, KH, FF, EE = V("klo", 0, 128), V("khi", 0, 128), V("khi", 128, 256), V("khi", 256, 384)
+        npa, nrelu = CFG["npa_last" if last else "npa"], CFG["nrelu"]
+        mm(KH, V("idp"), V("cst", 0, 128), True, False); mm(KH, V("idp"), V("cst", 256, 384), False, False)
+        mm(KL, V("idp"), V("cst", 0, 128), True, False); mm(KL, V("idp"), V("cst", 128, 256), False, False)
+        for k in range(4):
+            if k:
+                mm(V("s%d" % k), V("idp"), V("vv", 512 * k, 512 * k + 512), True, False)
+            mm(V("s%d" % k, 0, 256), V("idn"), z, False, False)
+            mm(V("s%d" % k, 256, 512), V("idn"), z, False, True)
+            act(V("ab", 2048 + 512 * k, 2560 + 512 * k), V("s%d" % k), Act.Abs)
+        rest = list(setup_rest()) if t == 0 else []
+        for c in range(8):
+            q = (c + t) % 8
+            tt(V("dd", 256 * c, 256 * c + 256), G(TAB(t), S("ru", t, 16 * q, 16 * q + 16)), z, Op.subtract)
+            if rest:
+                rest[c]()
+            if c % 2 and c - 1 > 8 - nrelu:
+                ts(V("ab", 256 * c - 768, 256 * c - 256), V("dd", 256 * c - 768, 256 * c - 256), 0.0, Op.max)
+        if CFG["db"]:
+            record("s", [TAB(t + 1)], [TAB(t), V("dd", 1024, 1280)], lambda a=ap(TAB(t + 1)), b=ap(TAB(t)): g.sync.dma_start(a, b),
+                   lambda p: 60.0, "m", (), lambda p: 4000.0)
+        if nrelu:
+            ts(V("ab", 1536, 2048), V("dd", 1536, 2048), 0.0, Op.max)
+        tt(VT(0), phi, plo, Op.subtract)
+
+        def low(k, stop):
+            if 4 * k >= 8 - nrelu:
+                sums("klo", 64 * k, 1024 * k, 4, "wp1", False, False, "dd")
+                sums("klo", 64 * k, 1024 * k, 4, "wn2", False, stop)
+            else:
+                act(V("ab", 1024 * k, 1024 * k + 512), V("dd", 1024 * k, 1024 * k + 512), Act.Abs)
+                act(V("ab", 1024 * k + 512, 1024 * k + 1024), V("dd", 1024 * k + 512, 1024 * k + 1024), Act.Abs)
+                sums("klo", 64 * k, 1024 * k, 4, "wneg", False, stop)
+        sums("khi", 0, 2048, 4, "wneg", False, False)
+        sums("khi", 64, 3072, 4, "wneg", False, False)
+        if nrelu == 8:
+            low(0, False)
+        mm(KH, V("idn"), J, False, False); mm(KH, V("idp"), Wm, False, True)
+        mm(KL, V("idn"), J, False, False); mm(KL, V("idn"), Wm, False, False)
+        mm(WmP, V("idp"), Wm, True, True)
+        if CFG["khs"] == "a" and nrelu == 8:
+            act(V("khs"), KH, Act.Copy)
+        else:
+            cp(V("khs"), KH)
+        if nrelu == 8:
+            low(1, True)
+        else:
+            low(nrelu // 4, False)
+            low(1 - nrelu // 4, True)
+        tt(V("m1", 0, 128), KL, V("khs"), Op.max)
+        tt(VT(3), V("khs"), KL, Op.subtract)
+        if t + 2 < ST:
+            send("ru", S("ru", t + 1), t + 2, [V("m1", 0, 128)])
+        if not last:
+            send("ra", S("rs", t, 0, 128), t + 1, [V("m1", 0, 128)])
+            send("rb", S("rs", t, 128, 256), t + 1, [V("m1", 0, 128)])
+        turned(128, t, 0)
+        turned(256, t, 128)
+        tt(V("m1", 128, 192), V("m1", 0, 64), V("m1", 64, 128), Op.max)
+        tt(V("m1", 192, 224), V("m1", 128, 160), V("m1", 160, 192), Op.max)
+        tt(V("m1", 224, 240), V("m1", 192, 208), V("m1", 208, 224), Op.max)
+        tt(V("x0"), G(V("m1", 224, 240), BC), J, Op.add)
+        ts(V("sp"), V("x0"), 14, Op.arith_shift_right, 1, Op.bitwise_and)
+        ts(V("jp"), V("x0"), 14336, Op.bitwise_and)
+        tt(VT(1), V("sp"), VT(0), Op.mult)
+        tt(V("x1"), V("x0"), WmP, Op.add)
+        tt(V("pf"), plo, VT(1), Op.add)
+        tt(VT(2), phi, VT(1), Op.subtract)
+        cp(V("pu"), V("pf"))
+        tt(V("m2", 0, 128), V("pf"), V("jp"), Op.add)
+        ts(V("sr"), V("x1"), 14, Op.arith_shift_right, 1, Op.bitwise_and)
+
+        PB = ["s0", "s1", "s3"]
+
+        def pgather(k):
+            act(V("vp", 512 * k, 512 * k + 512), G(TAB(t), V("pu", 32 * k, 32 * k + 32)), Act.Copy)
+
+        def psub(k):
+            mm(V(PB[k]), V("idp"), V("vp", 512 * k, 512 * k + 512), True, False)
+            mm(V(PB[k], 0, 256), V("idn"), V("yy"), False, False)
+            mm(V(PB[k], 256, 512), V("idn"), V("yy"), False, True)
+        right = [lambda: ts(V("thr"), V("jp"), 2048.0, Op.not_equal, LIM(0), Op.mult),
+                 lambda: tt(V("tq"), V("sr"), VT(3), Op.mult),
+                 lambda: tt(V("t2"), V("sr"), dR, Op.mult),
+                 lambda: tt(VT(3), V("tq"), KL, Op.add),
+                 lambda: tt(V("rf"), V("t2"), rlo, Op.add),
+                 lambda: tt(VT(0), V("thr"), VT(3), Op.is_gt)]
+
+        def filler(on=True):
+            if right and on:
+                right.pop(0)()
+        early = min(npa // 2, CFG["early"])
+        for k in range(early):
+            pgather(k)
+        tt(V("m2", 128, 192), V("m2", 0, 64), V("m2", 64, 128), Op.min)
+        filler(CFG["fill"] > 0)
+        tt(V("m2", 192, 224), V("m2", 128, 160), V("m2", 160, 192), Op.min)
+        filler(CFG["fill"] > 1)
+        tt(V("m2", 224, 240), V("m2", 192, 208), V("m2", 208, 224), Op.min)
+        filler(CFG["fill"] > 2)
+        cp(V("yu"), V("m2", 224, 240))
+        filler(CFG["fill"] > 3)
+        if CFG["y"] == "v":
+            cp(V("yy"), G(TAB(t), V("yu")))
+            mm(V("msc", 256, 512), V("idp"), V("yy"), True, False); mm(V("msc", 256, 512), V("idn"), z, False, True)
+            act(S("zo", t), V("msc", 256, 512), Act.Abs)
+        else:
+            tt(V("dz"), G(TAB(t), V("yu")), z, Op.subtract)
+            act(V("yy"), G(TAB(t), V("yu")), Act.Copy)
+            act(S("zo", t), V("dz"), Act.Abs)
+        if not last:
+            send("zz", S("zo", t), t + 1)
+        else:
+            store("s", T.yz[:], ap(S("zo", t)), S("zo", t))
+        sums("khi", 384, 0, 1, "wpos", True, True, "yy")
+        for k in range(early, npa // 2):
+            pgather(k)
+        if CFG["avg"] == "a" or last:
+            mm(V("msc", 0, 256), V("idp"), V("yy"), True, False); mm(V("msc", 0, 256), V("idp"), z, False, True)
+            act(V("hm"), V("msc", 0, 256), Act.Identity, MAGIC, 0.5 - 2.0 ** -11)
+            act(V("avg"), V("hm"), Act.Identity, -MAGIC)
+        else:
+            mm(V("msc", 0, 256), V("idh"), V("qtr"), True, False)
+            mm(V("msc", 0, 256), V("idh"), V("yy"), False, False); mm(V("msc", 0, 256), V("idh"), z, False, True)
+        for k in range(npa // 2):
+            psub(k)
+            act(V("abp", 512 * k, 512 * k + 512), V(PB[k]), Act.Abs)
+        cp(V("ui", 0, 16), V("khi", 384, 400))
+        ts(V("ui", 16, 32), V("ui", 0, 16), 7, Op.bitwise_and)
+        tt(V("ui", 32, 48), V("ui", 16, 32), V("base"), Op.add)
+        cp(V("uu"), V("ui", 32, 48))
+        if CFG["avg"] == "v" and not last:
+            ts(V("avg"), V("msc", 0, 256), MAGIC, Op.add, MAGIC, Op.subtract)
+        for c in range(npa, 8):
+            tt(V("dp", 256 * c, 256 * c + 256), G(TAB(t), V("pu", 16 * c, 16 * c + 16)), V("yy"), Op.subtract)
+            if c == 7 and CFG["prelu"]:
+                ts(V("abp", 1536, 2048), V("dp", 1536, 2048), 0.0, Op.max, 2.0, Op.mult)
+            elif c % 2:
+                act(V("abp", 256 * c - 256, 256 * c + 256), V("dp", 256 * c - 256, 256 * c + 256), Act.Abs)
+        for k in CFG["ford"]:
+            if k and CFG["prelu"]:
+                sums("khi", 224, 1536, 2, "wm1", True, False, "dp")
+            sums("khi", 128 + 64 * k, 1024 * k, 4, "wpos", not (k and CFG["prelu"]), True, "abp")
+        cp(G(TAB(t + 1), V("uu")), V("avg"))
+        if last:
+            store("s", T.yx[:], ap(TAB(t + 1)), TAB(t + 1), 6000.0)
+        else:
+            pregather(t + 1, 0)
+        act(V("sg"), FF, Act.Sign, LIM(1))
+        act(EE, V("sg"), Act.Relu, acc=V("cnt", 0, 1))
+        while right:
+            filler()
+        tt(V("prod"), G(V("rf"), SH1), V("pf"), Op.mult)
+        tt(V("wn"), V("sr"), VT(0), Op.not_equal)
+        ts(V("pa"), V("prod"), LIM(2), Op.add)
+        if not last:
+            cp(S("jo", t, 0, 128), V("jp"))
+            act(S("jo", t, 128, 256), G(V("wn"), SH1), Act.Identity, -2048.0, 16384.0)
+            send("jw", S("jo", t), t + 1)
+            mm(V("msc", 272, 273), V("blk"), V("cnt", 0, 1), True, True)
+            pregather(t + 1, 1, False)
+        tt(V("dlo"), VT(2), V("pf"), Op.subtract)
+        ts(V("new"), V("pa"), 5, Op.arith_shift_right, 2047, Op.bitwise_and)
+        tt(VT(1), V("dlo"), EE, Op.mult)
+        tt(V("dhi"), V("new"), VT(2), Op.subtract)
+        tt(S("po", t, 0, 128), V("pf"), VT(1), Op.add)
+        tt(V("ahi"), V("dhi"), EE, Op.mult)
+        if not last:
+            cp(V("ai", 0, 1), V("msc", 272, 273))
+        tt(S("po", t, 128, 256), V("ahi"), VT(2), Op.add)
+        if not last:
+            send("pa", S("po", t, 0, 128), t + 1)
+            send("pb", S("po", t, 128, 256), t + 1)
+            ts(V("ai", 1, 2), V("ai", 0, 1), 31, Op.bitwise_and)
+            ts(LIM(2), V("ai", 0, 1), 32.0, Op.mult)
+            pregather(t + 1, 2, False)
+            limits()
+            pregather(t + 1, 3, False)
+
+    seen.clear()
+    seen.update({q + k: 50 for q in "vat" for k in SCRATCH})
+    ts(V("coli", 4, 5), V("coli", 1, 2), 1, Op.arith_shift_right)
+    ts(V("coli", 5, 6), V("coli", 1, 2), 2, Op.arith_shift_right)
+    cp(C(8), V("coli", 4, 5)); cp(C(9), V("coli", 5, 6))
+    ts(B2, V("li", 72, 80), C(8), Op.add); ts(B3, V("li", 80, 88), C(9), Op.add)
+    ts(C(7), V("coli", 3, 4), 15.0, Op.mult, C(0), Op.add)
+    ts(INV1, V("li", 136, 152), C(7), Op.add)
+    act(V("td"), G(S("po", ST - 1), P1), Act.Identity, -32.0, 2048.0)
+    tt(V("t2"), V("wn"), dR, Op.mult)
+    act(V("tq"), dR, Act.Copy)
+    tt(V("ta", 0, 128), V("t2"), rlo, Op.add)
+    tt(VT(0), V("tq"), rlo, Op.add)
+    tt(V("ta", 128, 256), VT(0), V("t2"), Op.subtract)
+    for k, lst in enumerate((B1, B2, B3)):
+        ts(V("bits", 128 * k, 128 * k + 128), G(V("jp"), lst), 13 - k, Op.arith_shift_right, 1, Op.bitwise_and)
+    tt(V("tb"), G(V("ta"), PK), V("td"), Op.add)
+    cur, oth = "tb", "ta"
+    for k in range(3):
+        tt(VT(0), V(cur, 128, 256), V(cur, 0, 128), Op.subtract)
+        tt(VT(1), V("bits", 128 * k, 128 * k + 128), VT(0), Op.mult)
+        tt(V(oth, 0, 256, 2), V(cur, 0, 128), VT(1), Op.add)
+        tt(V(oth, 1, 256, 2), V(cur, 128, 256), VT(1), Op.subtract)
+        cur, oth = oth, cur
+    cp(V(oth), G(V(cur), INV1))
+    tr(V(cur), V(oth))
+    cp(V("ti"), G(V(cur), INV2))
+    act(V("td"), G(V(cur), INV2), Act.Identity, 2.0 ** -12 - 0.5, 2.0 ** -11)
+    ts(V("tj"), V("ti"), 2047, Op.bitwise_and)
+    act(V("te"), V("td"), Act.Identity, MAGIC)
+    cp(V("orr"), V("tj"))
+    act(V("op"), V("te"), Act.Identity, -MAGIC)
+    for (sp_, sc_, dp_, dc_) in blocks():
+        store("s", T.yr[dp_, dc_], T.orr[sp_, sc_], V("orr"))
+    for (sp_, sc_, dp_, dc_) in blocks():
+        store("a", T.yp[dp_, dc_], T.op[sp_, sc_], V("op"))
+    emit()
+    g.sync.wait_ge(T.sem.sto, cnt["sto"])
+    for s in ("sent", "cv", "ca", "ct", "cg") + (("cpy",) if CFG["db"] else ()):
+        g.wait_ge(T.sem[s], cnt[s])

@@ -2,9 +2,9 @@ import numpy as np
 from concourse.mybir import AluOpType as Op, ActivationFunctionType as Act
 
 ST = 6
-BIG = float(2 ** 27)
 MAGIC = float(3 * 2 ** 22)
-F, H, I, U = "float32", "bfloat16", "int32", "uint16"
+M8, M16 = 8 * MAGIC, 16 * MAGIC
+F, H, I, U, S16 = "float32", "bfloat16", "int32", "uint16", "float16"
 
 
 def _sb(n, d):
@@ -12,50 +12,43 @@ def _sb(n, d):
 
 
 SCRATCH = {
-    "tab": _sb(2048, H), "tab2": _sb(2048, H), "vv": _sb(2048, H), "dd": _sb(2048, H), "ab": _sb(4096, H),
-    "vp": _sb(2048, H), "dp": _sb(2048, H), "abp": _sb(2048, H), "t2": _sb(128, F),
+    "tab": _sb(2048, H), "vv": _sb(4096, H), "dd": _sb(4096, H), "ab": _sb(4096, H),
+    "vp": _sb(2048, H), "dp": _sb(2048, H), "abp": _sb(2048, H),
     "zz": _sb(256 * ST, H), "zo": _sb(256 * ST, H), "jw": _sb(256 * ST, H), "jo": _sb(256 * ST, H),
-    "pp": _sb(256 * ST, F), "po": _sb(256 * ST, F),
-    "ru": _sb(256 * ST, U), "rs": _sb(256 * ST, F), "idf": _sb(128, F), "idh": _sb(128, H), "qtr": _sb(256, H), "wn2": _sb(144, H), "wp1": _sb(144, H), "wm1": _sb(144, H),
-    "pin": _sb(256, I), "rin": _sb(256, I), "thi": _sb(4, I), "ta": _sb(256, F), "tb": _sb(256, F), "tc": _sb(512, F),
+    "pp": _sb(512 * ST, S16), "po": _sb(512 * ST, S16), "ru": _sb(256 * ST, U), "rs": _sb(256 * ST, S16),
+    "pin": _sb(256, I), "rin": _sb(256, I), "thi": _sb(4, I), "ta": _sb(256, F), "tb": _sb(256, F), "tc": _sb(256, F),
     "td": _sb(256, F), "te": _sb(256, F), "ti": _sb(256, I), "tj": _sb(256, I), "op": _sb(256, F), "orr": _sb(256, F),
     "col": _sb(16, F), "coli": _sb(8, I), "cidx": _sb(144, F), "blk": _sb(128, F), "blki": _sb(128, F),
-    "wneg": _sb(144, H), "wpos": _sb(144, H), "idp": _sb(128, H), "idn": _sb(128, H), "cst": _sb(384, H),
-    "li": _sb(160, I), "lh": _sb(48, I), "lr": _sb(48, I), "lu": _sb(160, U), "base": _sb(16, I), "q2": _sb(128, I),
-    "khs": _sb(128, F), "m1": _sb(256, F), "x0": _sb(128, I), "x1": _sb(128, I), "sp": _sb(128, I), "sr": _sb(128, I),
-    "jp": _sb(128, I), "pf": _sb(128, F), "m2": _sb(256, F), "yu": _sb(16, U), "pu": _sb(128, U),
-    "yy": _sb(256, H), "dz": _sb(256, H), "hm": _sb(256, F), "avg": _sb(256, H),
-    "ui": _sb(48, I), "uu": _sb(16, U), "thr": _sb(128, F), "tq": _sb(128, F), "wn": _sb(128, F), "rf": _sb(128, F),
-    "prod": _sb(128, F), "pa": _sb(128, I), "new": _sb(128, I), "dlo": _sb(128, F), "dhi": _sb(128, F), "ahi": _sb(128, F),
-    "sg": _sb(128, F), "cnt": _sb(4, F), "ai": _sb(8, I), "lim": _sb(16, F), "bits": _sb(512, I),
-    "s0": ("psum", [128, 512], F), "s1": ("psum", [128, 512], F), "s2": ("psum", [128, 512], F), "s3": ("psum", [128, 512], F),
-    "klo": ("psum", [128, 512], F), "khi": ("psum", [128, 512], F), "msc": ("psum", [128, 512], F), "vt": ("psum", [128, 512], F),
+    "wn64": _sb(144, H), "wp64": _sb(144, H), "wp1": _sb(144, H), "wn1": _sb(144, H), "ids": _sb(128 * 9, H),
+    "cst": _sb(128 * 5 + 256 + 16, H), "li": _sb(160, I), "lu": _sb(160, U), "base": _sb(16, I), "b16": _sb(16, S16), "q2": _sb(128, I),
+    "khs": _sb(128, F), "m1": _sb(256, F), "mi": _sb(32, I), "un": _sb(128, H), "sp": _sb(128, H), "rr": _sb(128, H),
+    "t3": _sb(128, S16), "pu": _sb(128, U), "mx": _sb(128, S16), "yu": _sb(16, U), "yy": _sb(256, H), "dz": _sb(256, H),
+    "avg": _sb(256, I), "r8": _sb(32, S16), "uu": _sb(16, U), "fl": _sb(256, H), "ww": _sb(128, H), "sr": _sb(128, H),
+    "t2": _sb(128, S16), "s1": _sb(128, H), "s3": _sb(128, H), "prod": _sb(128, F), "pa": _sb(128, I), "new": _sb(128, I),
+    "sg": _sb(128, H), "ee": _sb(128, H), "eb": _sb(128, H), "cnt": _sb(4, F), "ai": _sb(8, I), "lim": _sb(16, F),
+    "jp": _sb(64, I), "bits": _sb(768, H), "xp": _sb(1024, S16), "xr": _sb(1024, S16),
 }
-STREAMS = {"ru": ("ru", 0, 256), "ra": ("rs", 0, 128), "rb": ("rs", 128, 256), "zz": ("zz", 0, 256), "jw": ("jw", 0, 256),
-           "pa": ("pp", 0, 128), "pb": ("pp", 128, 256)}
-CFG = {"npa": 6, "npa_last": 6, "nrelu": 4, "khs": "a", "early": 2, "fill": 4, "y": "v", "avg": "v", "db": 0, "inorder": "", "phase": 1, "prelu": 0, "ford": (0, 1)}
-PAR = {"c": 1.0, "g": 1.5, "scat": 3.8, "fix": 30.0, "pe": 0.5, "wake": 100.0, "issue": 400.0, "hop": 4500.0, "w": 2 / 120}
-PARS = [PAR, dict(PAR, g=1.04, scat=1.6, wake=50.0, hop=3000.0, w=1 / 100), dict(PAR, g=2.08, scat=6.0, wake=200.0, pe=0.83, hop=5500.0, w=1 / 160),
-        dict(PAR, hop=2500.0, fix=60.0, pe=0.42, wake=150.0, w=1 / 120)]
-TRIES = [3000, 1, 1.0]
-MOVED = {x.split(":")[0]: 100 * int(x.split(":")[1]) for x in (
-    "aab2:-1 aab6:-10 aabp1:5 aabp2:21 aabp3:-5 aabp4:19 ajo1:6 asg1:-10 avp1:-8 avp3:44 avv1:6 avv3:-8 avv4:-7 avv5:-4 awn21:42 "
-    "azo1:3 gjo1:-10 gli2:34 gpo1:2 gq21:75 gzo1:9 laab5:-1 laabp3:-3 lakhi1:-2 lasg1:-10 ltkhi5:-10 ltkhi6:-10 ltkhi7:-10 ltklo6:-2 "
-    "ltklo7:-9 lts05:-10 lts16:-10 lts34:6 lts35:3 lvahi1:-4 lvdd1:-2 lvdd2:19 lvdhi1:3 lvdlo1:13 lvm21:-10 lvm23:-10 lvnew1:-10 "
-    "lvpo2:-1 lvprod1:20 lvrf1:2 lvsr1:-10 lvt21:-10 lvtq1:-10 lvvt1:-5 lvvt3:65 lvvt4:5 lvvt5:-6 lvx01:-4 lvx11:2 lvyy1:1 tkhi2:26 "
-    "tklo5:5 tklo6:-5 tklo7:1 tmsc1:22 tmsc2:67 ts01:-10 ts03:10 ts06:12 ts15:24 ts21:3 vab2:-7 vahi1:-2 vavg1:5 vcol52:28 vcoli2:57 "
-    "vdhi1:-10 vdp1:73 vdp2:80 vkhs1:7 vm12:-9 vm13:-3 vm14:-7 vm21:100 vpo2:-10 vpp1:16 vpu1:66 vsp1:-8 vt21:4 vt251:-1 vuu1:38 "
-    "vvt2:27 vvt5:19 vvt6:49 vvt7:-9 vx01:-10 vx11:31").split()}
+for _b in ("s0", "s2", "s4", "klo", "khi", "b5", "b6", "b7"):
+    SCRATCH["p" + _b] = ("psum", [128, 512], F)
+STAGE = ["ps0", "ps2"]
+IDS = [1.0, -1.0, 0.5, -0.5, 8.0, -8.0, 1024.0, -1024.0, -2.0]
+STREAMS = {"ru": ("ru", 256, 0, 256), "rs": ("rs", 256, 0, 256), "pa": ("pp", 512, 0, 128), "zz": ("zz", 256, 0, 256),
+           "jw": ("jw", 256, 0, 256), "pb": ("pp", 512, 128, 512)}
+CFG = {"d": "vvvmaaaa", "f": "aamv", "flast": "aaam", "d0": "vvvvaaaa", "e": "v", "y": "v", "quads": (0, 2, 3, 1)}
+PAR = {"c": 1.0, "g": 1.5, "scat": 3.8, "fix": 30.0, "pe": 0.5, "wake": 100.0, "issue": 400.0, "hop": 3400.0, "w": 2 / 120}
+PARS = [PAR, dict(PAR, g=1.04, scat=1.6, wake=50.0, hop=3000.0, w=1 / 100),
+        dict(PAR, g=2.08, scat=6.0, wake=200.0, pe=0.63, hop=5500.0, w=1 / 160)]
+TRIES = [300, 1, 1.0, 22000]
 PLAN = {}
 ORDER = [("ru", 1)] + [x for t in range(1, ST) for x in (
-    ("ru", t + 1), ("ra", t), ("rb", t), ("zz", t), ("jw", t), ("pa", t), ("pb", t)) if x[1] < ST]
+    ("ru", t + 1), ("rs", t), ("pa", t), ("zz", t), ("jw", t), ("pb", t)) if x[1] < ST]
 
 
 def relay_of(s, t):
-    return {"ru": 2 * (1 - t % 2), "zz": 0, "ra": 3, "rb": 1, "jw": 3, "pa": 2, "pb": 1}[s]
+    return {"ru": 2 * (1 - t % 2), "zz": 0, "rs": 1 + 2 * (t % 2), "jw": 3, "pa": 1, "pb": 2}[s]
 
 
-SEMAPHORES = (["cv", "ca", "ct", "cg", "ldr", "ldx", "ldz", "ldp", "sto", "sent", "cpy"]
+SEMAPHORES = (["cv", "ca", "ct", "cg", "ldr", "ldx", "ldz", "ldp", "sto", "sent"]
               + ["a%s%d" % (s, t) for s in STREAMS for t in range(1, ST)])
 
 
@@ -68,8 +61,8 @@ def relays(T, topo, rank):
 
 
 def slot(T, s, t):
-    name, a, b = STREAMS[s]
-    return T[name][:, 256 * t + a:256 * t + b]
+    name, w, a, b = STREAMS[s]
+    return T[name][:, w * t + a:w * t + b]
 
 
 def relay_program(g, core, T, topo):
@@ -91,6 +84,85 @@ def relay_program(g, core, T, topo):
         g.wait_ge(T.sem.sent, sent)
 
 
+def improve(ops, order, tries):
+    m, rng, K = len(ops), np.random.RandomState(0), range(len(PARS))
+    qs = [o["q"] for o in ops]
+    pre = [[[(j, ops[j]["ls"][k] + PARS[k]["wake"]) for j in o["wait"]]
+            + [(j, ops[j]["ls"][k]) for j in o["order"] if o["q"] == "x"] for o in ops] for k in K]
+    dep = [set(o["wait"]) | set(o["order"]) for o in ops]
+    same = {}
+    for i, o in enumerate(ops):
+        same.setdefault(o["id"], []).append(i)
+
+    def times(od, k):
+        end, free, why, pk, top = [0.0] * m, {}, [-1] * m, pre[k], (0.0, 0)
+        for i in od:
+            t0, w = free.get(qs[i], (0.0, -1))
+            for j, d in pk[i]:
+                if end[j] + d >= t0:
+                    t0, w = end[j] + d, j
+            end[i], why[i] = t0 + ops[i]["cs"][k], w
+            if qs[i] != "x":
+                free[qs[i]] = (end[i], i)
+            if end[i] + ops[i]["ls"][k] > top[0]:
+                top = (end[i] + ops[i]["ls"][k], i)
+        return top[0], why, top[1]
+
+    def score(od):
+        r = [times(od, k) for k in K]
+        return sum(r[k][0] * PARS[k]["w"] for k in K), r
+
+    def move(od, i, j):
+        a, b = od.index(j), od.index(i)
+        need, queues, first = {i}, set(), []
+        for x in reversed(od[a:b + 1]):
+            if x in need or qs[x] in queues:
+                if x == j:
+                    return od
+                first.append(x)
+                need |= dep[x]
+                if qs[x] != "x" and x != i:
+                    queues.add(qs[x])
+        fs = set(first)
+        return od[:a] + first[::-1] + [x for x in od[a:b + 1] if x not in fs] + od[b + 1:] if a < b else od
+
+    now = best = score(order)
+    cur = order
+    for n in range(tries):
+        _, why, i = now[1][rng.randint(len(PARS))]
+        pairs = []
+        while why[i] >= 0:
+            if qs[why[i]] == qs[i] and why[i] not in dep[i]:
+                pairs.append((i, why[i]))
+            i = why[i]
+        if not pairs:
+            break
+        i, j = pairs[rng.randint(len(pairs))]
+        u = rng.rand()
+        if u < 0.5:
+            qq = [x for x in cur if qs[x] == qs[i]]
+            k = qq.index(j)
+            if u < 0.25:
+                j = qq[max(0, k - rng.randint(4))]
+            else:
+                i = qq[min(len(qq) - 1, k + 1 + rng.randint(4))]
+        todo = [(i, j)]
+        if rng.rand() < 0.6:
+            si, sj = same[ops[i]["id"]], same[ops[j]["id"]]
+            d = si.index(i) - sj.index(j)
+            todo = [(si[k], sj[k - d]) for k in range(len(si)) if 0 <= k - d < len(sj)]
+        od = cur
+        for a, b in todo:
+            od = move(od, a, b)
+        if od is not cur:
+            x = score(od)
+            if x[0] <= now[0] + 5.0 * (1 - n / tries) * rng.exponential():
+                cur, now = od, x
+                if x[0] < best[0]:
+                    best, order = x, od
+    return order, (best[0], [r[0] for r in best[1]])
+
+
 def rank_program(g, core, T, topo):
     rank = T.rank_of(core)
     if rank is None:
@@ -101,13 +173,16 @@ def rank_program(g, core, T, topo):
 
     Q = {"v": g.vector, "a": g.scalar, "t": g.tensor, "g": g, "s": g.sync}
     SEM = {"v": "cv", "a": "ca", "t": "ct", "g": "cg"}
-    cnt = {"cv": 0, "ca": 0, "ct": 0, "cg": 0, "sent": 0, "sto": 0, "cpy": 0}
+    cnt = {"cv": 0, "ca": 0, "ct": 0, "cg": 0, "sent": 0, "sto": 0}
     known = {q: {} for q in Q}
     hist = {}
     psum = [k for k in SCRATCH if SCRATCH[k][0] == "psum"]
 
     def V(name, a=0, b=None, step=1):
         return (name, a, SCRATCH[name][1][1] if b is None else b, step)
+
+    def sub(v, a, b):
+        return (v[0], v[1] + a, v[1] + b, 1)
 
     def G(win, off):
         return ("ind", win, off)
@@ -138,9 +213,9 @@ def rank_program(g, core, T, topo):
             return 55 + m * PAR["g"] * PAR["c"]
         full = [v for v in vs if size(v) == m]
         per = 1.0
-        if q == "v" and len(full) == 2 and not any(v[0] in psum for v in full):
-            per = 2.0
-        elif q == "v" and all(SCRATCH[v[0]][2] in (H, U) for v in full + [o]):
+        if q == "v" and len(full) == 2:
+            per = 1.0 if any(v[0] in psum for v in full) else 2.0
+        elif q == "v" and all(SCRATCH[v[0]][2] in (H, U, S16) for v in full + [o]):
             per = 0.5
         return PAR["fix"] + max(64, m * per) * PAR["c"]
 
@@ -167,7 +242,7 @@ def rank_program(g, core, T, topo):
                     if v[3] == 2 and v[1] == a + 1 and k2 == "w" and i == me - 1:
                         continue
                     if not (q == "t" and q2 == "t") and a < v[2] and v[1] < b and (kd == "w" or k2 == "w"):
-                        (order if kd == "w" and q == q2 and q in CFG["inorder"] else wait).add(i)
+                        wait.add(i)
         for name in set(v[0] for v in wr + rd if v[0] in psum):
             bk = banks.setdefault(name, {"q": q, "now": [], "was": [], "pe": []})
             if bk["q"] != q:
@@ -184,7 +259,7 @@ def rank_program(g, core, T, topo):
                     "kind": kind, "wait": sorted(wait), "order": sorted(order), "tok": tok})
         for v in wr:
             hist[v[0]] = [e for e in hist.get(v[0], []) if not (v[1] <= e[0] and e[1] <= v[2])] + [(v[1], v[2], "w", q, me)]
-        for v in rd if kind in "cm" else []:
+        for v in rd if kind == "c" else []:
             hist[v[0]] = hist.get(v[0], []) + [(v[1], v[2], "r", q, me)]
         return me
 
@@ -213,10 +288,9 @@ def rank_program(g, core, T, topo):
     def best_plan():
         rng = np.random.RandomState(TRIES[1])
         ids = sorted(o["id"] for o in ops if o["q"] in "vatg")
-        boost = dict(MOVED)
+        boost = {}
         order = plan(boost)
         best = now = length(order)
-        kept = boost
         for it in range(TRIES[0]):
             b = dict(boost)
             for _ in range(1 + int(rng.randint(3))):
@@ -228,8 +302,9 @@ def rank_program(g, core, T, topo):
             if x[0] <= now[0] + TRIES[2] * (1.0 - it / TRIES[0]) * rng.exponential():
                 boost, now = b, x
                 if x[0] <= best[0]:
-                    kept, order, best = b, od, x
-        PLAN.update(length=best, kept=kept, plan=plan, weigh=length)
+                    order, best = od, x
+        order, best = improve(ops, order, TRIES[3])
+        PLAN.update(length=best, ops=ops)
         return order
 
     def plan(boost):
@@ -289,10 +364,6 @@ def rank_program(g, core, T, topo):
                 cnt[SEM[q]] += 1
                 o["call"]().then_inc(T.sem[SEM[q]], 1)
                 o["tok"] = (SEM[q], cnt[SEM[q]], dict(k))
-            elif o["kind"] == "m":
-                cnt["cpy"] += 16
-                o["call"]().then_inc(T.sem.cpy, 16)
-                o["tok"] = ("cpy", cnt["cpy"], dict(k))
             else:
                 o["call"]()
 
@@ -324,6 +395,28 @@ def rank_program(g, core, T, topo):
     def mm(o, w, x, start, stop):
         run("t", [o], [w, x], lambda: g.tensor.matmul(ap(o), ap(w), ap(x), start, stop))
 
+    def ID(x):
+        k = IDS.index(x)
+        return V("ids", 128 * k, 128 * k + 128)
+
+    def lin(o, terms, start=True, stop=True):
+        m = o[2] - o[1]
+        terms = [(x[0], x[1], x[2] % m if len(x) > 2 else 0) for x in terms]
+        terms.sort(key=lambda x: x[2] > 0)
+        if terms[0][2] == 0 or not start:
+            groups = [[(x, y, a, b, (a + r) % m) for x, y, r in terms for a, b in ((0, m - r), (m - r, m)) if a < b]]
+        else:
+            cuts = sorted(set([0, m] + [m - r for _, _, r in terms]))
+            groups = [[(x, y, a, b, (a + r) % m) for x, y, r in terms] for a, b in zip(cuts, cuts[1:])]
+
+        def call():
+            for gr in groups:
+                for k, (x, y, a, b, c) in enumerate(gr):
+                    last = g.tensor.matmul(ap(sub(o, a, b)), ap(ID(x)), ap(sub(y, c, c + b - a)), start and k == 0, stop and k == len(gr) - 1)
+            return last
+        record("t", [o], [ID(x) for x in set(x[0] for x in terms)] + [x[1] for x in terms], call,
+               lambda p: sum(max(64, e[3] - e[2]) for gr in groups for e in gr) * p["pe"])
+
     def iota(o, pat, base=0, cm=0):
         if SCRATCH[o[0]][2] == I:
             run("g", [o], [], lambda: g.iota(ap(o), pat, base, cm))
@@ -339,57 +432,49 @@ def rank_program(g, core, T, topo):
         cnt["sent"] += len(topo.engines(core, to))
         me = record("g", [], [src] + list(after), lambda: g.remote_dma(
             slot(T, s, t), ap(src), T.sem["a%s%d" % (s, t)], T.sem.sent, pid, rid, topo.mask(core, to)),
-            lambda p: p["issue"], "r", [sends["last"]] if sends else [], lambda p: p["hop"])
+            lambda p: p["issue"], "r", [sends["last"]] if sends else [], lambda p: p["hop"] + (600.0 if s == "pb" else 0.0))
         assert ORDER[sends.get("n", 0)] == (s, t)
         sends.update(last=me, n=sends.get("n", 0) + 1)
-        landed(S(STREAMS[s][0], t, STREAMS[s][1], STREAMS[s][2]), "a%s%d" % (s, t), len(topo.engines(rl_in[relay_of(s, t)] if rl_in else prv, core)), 0.0, [me])
+        name, w, a, b = STREAMS[s]
+        landed(V(name, w * t + a, w * t + b), "a%s%d" % (s, t), len(topo.engines(rl_in[relay_of(s, t)] if rl_in else prv, core)), 0.0, [me])
 
     def store(q, dst, src, v, lat=2200.0):
         cnt["sto"] += 16
         record(q, [], [v], lambda: Q[q].dma_start(dst, src).then_inc(T.sem.sto, 16), lambda p: 100.0, "d", (), lambda p: lat)
 
+
     def blocks():
         for gg in range(4):
             for x in range(2):
-                for y in range(2):
-                    yield (slice(32 * gg + 16 * x, 32 * gg + 16 * x + 16), slice(128 * y, 128 * y + 128),
-                           slice(32 * gg + 16 * y, 32 * gg + 16 * y + 16), slice(128 * x, 128 * x + 128))
+                yield slice(32 * gg, 32 * gg + 32), slice(128 * x, 128 * x + 128), slice(32 * gg + 16 * x, 32 * gg + 16 * x + 16)
 
     def S(name, t, a=0, b=None):
-        return V(name, 256 * t + a, 256 * t + (256 if b is None else b))
+        w = SCRATCH[name][1][1] // ST
+        return V(name, w * t + a, w * t + (w if b is None else b))
 
-    for k, (sp_, sc_, dp_, dc_) in enumerate(blocks()):
-        Q["sa"[k % 2]].dma_start(T.rin[sp_, sc_], T.pr[dp_, dc_]).then_inc(T.sem.ldr, 16)
+    for k, (sp_, sc_, rows) in enumerate(blocks()):
+        Q["sa"[k % 2]].dma_start(T.rin[sp_, sc_], T.pr[rows, :]).then_inc(T.sem.ldr, 16)
     g.sync.dma_start(T.tab[:], T.xt[:]).then_inc(T.sem.ldx, 16)
     g.scalar.dma_start(T.zz[:, 0:256], T.z0[:]).then_inc(T.sem.ldz, 16)
     g.scalar.dma_start(T.thi[:, 0:1], T.th[:], ).then_inc(T.sem.ldz, 16)
-    for (sp_, sc_, dp_, dc_) in blocks():
-        g.sync.dma_start(T.pin[sp_, sc_], T.pl[dp_, dc_]).then_inc(T.sem.ldp, 16)
-    landed(V("rin"), "ldr", 256, 2500.0); landed(V("tab"), "ldx", 16, 4500.0); landed(S("zz", 0), "ldz", 32, 3000.0)
-    landed(V("thi"), "ldz", 32, 3000.0); landed(V("pin"), "ldp", 256, 4500.0)
+    for (sp_, sc_, rows) in blocks():
+        g.sync.dma_start(T.pin[sp_, sc_], T.pl[rows, :]).then_inc(T.sem.ldp, 16)
+    landed(V("rin"), "ldr", 128, 2500.0); landed(V("tab"), "ldx", 16, 4300.0); landed(S("zz", 0), "ldz", 32, 4300.0)
+    landed(V("thi"), "ldz", 32, 4300.0); landed(V("pin"), "ldp", 128, 4800.0)
 
     def C(k):
         return V("col", k, k + 1)
-    P1, BC, INV2, SH1, PK, B1, B2, B3, P2, INV1 = [V("lu", a, b) for a, b in (
-        (0, 16), (16, 24), (24, 40), (40, 48), (48, 64), (64, 72), (72, 80), (80, 88), (120, 136), (136, 152))]
-
-    def TAB(t):
-        return V("tab2" if CFG["db"] and t % 2 else "tab")
+    P1, BC, BC16, INV2, P2 = [V("lu", a, b) for a, b in ((0, 16), (16, 24), (16, 32), (32, 48), (120, 136))]
+    C33, C7, C1, C32, C0, QTR, M35 = [V("cst", a, b) for a, b in (
+        (0, 128), (128, 256), (256, 384), (384, 512), (512, 640), (640, 896), (896, 912))]
+    TAB = V("tab")
     iota(V("coli", 0, 1), [[0, 1]], 0, 1)
     iota(V("li", 0, 16), [[16, 8], [128, 2]])
-    iota(V("li", 120, 136), [[1, 16]])
+    iota(V("li", 120, 136), [[2, 16]])
     iota(V("cidx"), [[1, 144]])
-    iota(V("q2"), [[2048, 8], [0, 16]])
-    iota(V("li", 16, 24), [[0, 8]])
-    iota(V("li", 24, 40), [[16, 2], [32, 8]])
-    iota(V("lr", 0, 8), [[16, 8]], 16)
-    iota(V("lr", 8, 24), [[16, 8], [0, 2]], 16)
-    iota(V("lh", 0, 8), [[0, 8]])
-    iota(V("lh", 8, 24), [[0, 8], [128, 2]])
-    iota(V("li", 64, 72), [[16, 4], [0, 2]])
-    iota(V("li", 72, 80), [[16, 2], [0, 2], [8, 2]])
-    iota(V("li", 80, 88), [[0, 2], [4, 4]])
-    iota(V("li", 136, 152), [[8, 8], [64, 2]])
+    iota(V("q2"), [[2, 8], [0, 16]])
+    iota(V("li", 16, 32), [[0, 16]])
+    iota(V("li", 32, 48), [[16, 2], [32, 8]])
     iota(V("base"), [[128, 16]])
     iota(V("blki"), [[16, 8], [0, 16]])
 
@@ -399,35 +484,40 @@ def rank_program(g, core, T, topo):
     cp(C(0), V("coli", 1, 2))
     ts(C(1), V("coli", 2, 3), 32.0, Op.mult)
     ts(P1, V("li", 0, 16), C(0), Op.add)
-    ts(C(2), V("coli", 3, 4), 2.0, Op.mult, C(1), Op.add)
+    ts(C(2), V("coli", 3, 4), 0.125, Op.mult, C(1), Op.add)
     cp(C(3), V("coli", 0, 1))
     ts(P2, V("li", 120, 136), C(2), Op.add)
     ts(C(4), C(3), C(0), Op.subtract)
-    ts(V("idp"), V("cidx", 0, 128), C(3), Op.is_equal)
+    ts(ID(1.0), V("cidx", 0, 128), C(3), Op.is_equal)
     ts(C(5), C(4), 15.0, Op.add)
-    ts(V("idn"), V("cidx", 0, 128), C(3), Op.is_equal, -1.0, Op.mult)
-    ts(V("wneg"), V("cidx"), C(5), Op.is_equal, -32768.0, Op.mult)
+    ts(V("wp1"), V("cidx"), C(5), Op.is_equal)
+    for x in IDS[1:]:
+        act(ID(x), ID(1.0), Act.Identity, 0.0, x)
+    for w, x in (("wn64", -64.0), ("wp64", 64.0), ("wn1", -1.0)):
+        act(V(w), V("wp1"), Act.Identity, 0.0, x)
+    for v, x in ((C33, 33.0), (C7, 7.0), (C1, 1.0), (C32, 32.0), (C0, 0.0), (M35, -3.5)):
+        ms(v, x)
     cp(V("ta"), G(V("rin"), P1))
-    ms(V("cst", 0, 128), BIG)
     tr(V("tb"), V("ta"))
-    ms(V("cst", 128, 256), -2048.0)
     cp(S("ru", 0), G(V("tb"), P2))
     send("ru", S("ru", 0), 1)
-    ms(V("cst", 256, 384), -14336.0)
-    act(V("wn2"), V("wneg"), Act.Identity, 0.0, 2.0)
-    act(V("wp1"), V("wneg"), Act.Identity, 0.0, -1.0)
-    act(V("wpos"), V("wneg"), Act.Identity, 0.0, -2.0 ** -15)
-    act(V("wm1"), V("wneg"), Act.Identity, 0.0, 2.0 ** -15)
-    act(V("idf"), V("idp"), Act.Copy)
-    act(V("idh"), V("idp"), Act.Identity, 0.0, 0.5)
-    ms(V("qtr"), -0.5)
+    cp(S("rs", 0), S("ru", 0))
+    cp(V("td"), G(V("pin"), P1))
+    tr(V("te"), V("td"))
+    cp(S("pp", 0, 0, 256), G(V("te"), P2))
+    cp(S("jw", 0, 0, 128), V("q2"))
+    ms(S("jw", 0, 128, 256), -1.0)
+    act(C(6), C(0), Act.Identity, 0.0, 8.0)
+    ts(V("lu", 16, 48), V("li", 16, 48), C(0), Op.add)
+    ts(V("b16"), V("base"), C(6), Op.add)
+    ts(V("blk"), V("blki"), C(4), Op.is_equal, -32.0, Op.mult)
 
     def LIM(k):
         return V("lim", k, k + 1)
+    ts(LIM(0), V("thi", 0, 1), -1.0, Op.mult, -0.125, Op.add)
+    act(LIM(1), LIM(0), Act.Copy)
 
-    def sums(bank, o, src, rows, w, start, stop, buf="ab"):
-        out = V(bank, o, o + 16 * rows)
-
+    def sums(out, w, buf, src, rows, start, stop):
         def call():
             for a in range(16):
                 last = g.tensor.matmul(ap(out), ap(V(w, 15 - a, 143 - a)), ap(V(buf, src + a, src + 256 * rows, 16)),
@@ -435,269 +525,233 @@ def rank_program(g, core, T, topo):
             return last
         record("t", [out], [V(w), V(buf, src, src + 256 * rows)], call, lambda p: 16 * max(64, 16 * rows) * p["pe"])
 
-    def pregather(t, k, into=True):
-        q = (2 * k + t) % 8
-        if q == 7:
-            act(V("vv", 512 * k, 512 * k + 256), G(TAB(t), S("ru", t, 240, 256)), Act.Copy)
-            act(V("vv", 512 * k + 256, 512 * k + 512), G(TAB(t), S("ru", t, 128, 144)), Act.Copy)
+    def rnames(t, row, k=1):
+        c = 128 * (row // 8) + 16 * ((row + t) % 8)
+        return S("ru", t, c, c + 16 * k)
+
+    def ahead(t, kinds):
+        for c in range(8):
+            if kinds[c] in "ab":
+                parts = [(0, 1), (1, 1)] if (2 * c + t) % 8 == 7 else [(0, 2)]
+                for r, k in parts:
+                    o, src = V("vv", 512 * c + 256 * r, 512 * c + 256 * (r + k)), G(TAB, rnames(t, 2 * c + r, k))
+                    if kinds[c] == "a":
+                        act(o, src, Act.Copy)
+                    else:
+                        cp(o, src)
+
+    stage = [0]
+
+    def sizes(kind, c, names, z, raw, dif, out):
+        o = V(out, 512 * c, 512 * c + 512)
+        if kind in "ab":
+            bk = STAGE[stage[0] % len(STAGE)]
+            stage[0] += 1
+            mm(V(bk), ID(1.0), V(raw, 512 * c, 512 * c + 512), True, False)
+            mm(V(bk, 0, 256), ID(-1.0), z, False, False)
+            mm(V(bk, 256, 512), ID(-1.0), z, False, True)
+            act(o, V(bk), Act.Abs)
+            return
+        for r in range(2):
+            tt(V(dif, 512 * c + 256 * r, 512 * c + 256 * r + 256), G(TAB, names(2 * c + r)), z, Op.subtract)
+        if kind == "v":
+            ts(o, V(dif, 512 * c, 512 * c + 512), 0.0, Op.max, 2.0, Op.mult)
         else:
-            act(V("vv", 512 * k, 512 * k + 512), G(TAB(t), S("ru", t, 128 + 16 * q, 160 + 16 * q)), Act.Copy)
-        if into:
-            mm(V("s%d" % k), V("idp"), V("vv", 512 * k, 512 * k + 512), True, False)
+            act(o, V(dif, 512 * c, 512 * c + 512), Act.Abs)
 
-    def turned(o, t, half):
-        c = 128 - 16 * t
-        mm(V("s2", o, o + c), V("idf"), S("rs", t, half + 16 * t, half + 128), True, True)
-        if t:
-            mm(V("s2", o + c, o + 128), V("idf"), S("rs", t, half, half + 16 * t), True, True)
+    def quad(kinds, k, out, wabs, wdif, ab, dif, stop):
+        vs = [c for c in (2 * k, 2 * k + 1) if kinds[c] == "v"]
+        if vs:
+            a = 32 * (vs[0] - 2 * k)
+            sums(sub(out, a, a + 32 * len(vs)), wdif, dif, 512 * vs[0], 2 * len(vs), False, False)
+        sums(out, wabs, ab, 1024 * k, 4, False, stop)
 
-    def limits():
-        ts(LIM(0), V("ai", 1, 2), -32768.0, Op.mult, LIM(4), Op.add)
-        ts(LIM(1), V("ai", 1, 2), -1.0, Op.mult, LIM(5), Op.add)
+    KEYS = [V(bk, 0, 64) for bk in ("pb7", "pb6", "pkhi", "pklo")]
+    X, WX = V("pklo", 128, 256), V("pklo", 256, 384)
+    JP, FF = V("pkhi", 128, 256), V("pkhi", 256, 384)
+    DP, PL, YS, UU = V("pb5", 0, 128), V("pb5", 128, 256), V("pb5", 256, 272), V("pb5", 272, 288)
+    DLO, PS, EP, CNT = V("ps4", 0, 128), V("ps4", 128, 256), V("ps4", 256, 384), V("ps4", 384, 385)
+    DR, AB, RF, S2 = [V("pb6", 128 * k, 128 * k + 128) for k in range(4)]
+    DZ, AVG = V("pb7", 0, 256), V("pb7", 256, 512)
 
-    for k in range(4):
-        pregather(0, k, k == 0)
+    def in_order(x, bks, tmp, out, dst, queues):
+        open_ = len(set(bks)) == 4
 
-    def VT(k):
-        return V("vt", 128 * k, 128 * k + 128)
+        def add(k, j, start, stop):
+            o, src, r = V(bks[k], 0, 256), V(x, 256 * j, 256 * j + 256), 64 >> k
+            todo = [(1.0, 0, 256, 0)] if k == 3 else [(-1.0, 0, 256, 0)] + [
+                (1.0, h + a, h + b, h + (a - r) % 128) for h in (0, 128) for a, b in ((0, r), (r, 128))]
 
-    def setup_rest():
-        yield lambda: cp(V("tc", 0, 256), S("ru", 0))
-        yield lambda: cp(V("td"), G(V("pin"), P1))
-        yield lambda: (tt(S("rs", 0, 128, 256), V("tc", 128, 256), V("tc", 0, 128), Op.subtract),
-                       ts(S("rs", 0, 0, 128), V("tc", 0, 128), 32.0, Op.add))
-        yield lambda: (tr(V("te"), V("td")), cp(S("jw", 0, 0, 128), V("q2")))
-        yield lambda: (ms(S("jw", 0, 128, 256), -2048.0), ts(V("lr", 0, 24), V("lr", 0, 24), 127, Op.bitwise_and))
-        yield lambda: (cp(S("pp", 0), G(V("te"), P2)), tt(V("li", 40, 64), V("lr", 0, 24), V("lh", 0, 24), Op.add), act(C(6), C(0), Act.Identity, 0.0, 8.0))
-        yield lambda: (cp(LIM(3), V("thi", 0, 1)), ms(LIM(2), 0.0), ts(V("lu", 16, 72), V("li", 16, 72), C(0), Op.add),
-                       ts(V("base"), V("base"), C(6), Op.add),
-                       act(LIM(4), LIM(3), Act.Identity, BIG - 31744.0, -32768.0), act(LIM(5), LIM(3), Act.Identity, -0.5, -1.0),
-                       act(LIM(0), LIM(4), Act.Copy), act(LIM(1), LIM(5), Act.Copy))
-        yield lambda: ts(V("blk"), V("blki"), C(4), Op.is_equal)
+            def call():
+                for i, (f, a, b, c) in enumerate(todo):
+                    res = g.tensor.matmul(ap(sub(o, a, b)), ap(ID(f)), ap(sub(src, c, c + b - a)), start and i == 0, stop and i == len(todo) - 1)
+                return res
+            record("t", [o], [ID(1.0), ID(-1.0), src], call, lambda p: sum(max(64, e[2] - e[1]) for e in todo) * p["pe"])
+        for k in range(4):
+            if open_:
+                for k2 in range(k, 4):
+                    add(k2, k, k == 0, k2 == k)
+            else:
+                for j in range(k + 1):
+                    add(k, j, j == 0, j == k)
+            if k < 3:
+                tt(V(x, 256 * k + 256, 256 * k + 512), V("bits", 512 - 256 * k, 768 - 256 * k), V(bks[k], 0, 256), Op.mult)
+        for b in range(8):
+            tr(V(tmp, 32 * b, 32 * b + 32), V(bks[3], b, 256, 8))
+        act(V(out), G(V(tmp), INV2), Act.Copy)
+        for k, (sp_, sc_, rows) in enumerate(blocks()):
+            store(queues[k % len(queues)], dst[rows, :], T[out][sp_, sc_], V(out))
 
+    ahead(0, CFG["d0"])
     for t in range(ST):
         last = t == ST - 1
         seen.clear()
-        seen["phase"] = "l" if last and CFG["phase"] else ""
-        z, J, Wm = S("zz", t), S("jw", t, 0, 128), S("jw", t, 128, 256)
-        plo, phi = S("pp", t, 0, 128), S("pp", t, 128, 256)
-        WmP, rlo, dR = V("s2", 0, 128), V("s2", 128, 256), V("s2", 256, 384)
-        KL, KH, FF, EE = V("klo", 0, 128), V("khi", 0, 128), V("khi", 128, 256), V("khi", 256, 384)
-        npa, nrelu = CFG["npa_last" if last else "npa"], CFG["nrelu"]
-        mm(KH, V("idp"), V("cst", 0, 128), True, False); mm(KH, V("idp"), V("cst", 256, 384), False, False)
-        mm(KL, V("idp"), V("cst", 0, 128), True, False); mm(KL, V("idp"), V("cst", 128, 256), False, False)
-        for k in range(4):
-            if k:
-                mm(V("s%d" % k), V("idp"), V("vv", 512 * k, 512 * k + 512), True, False)
-            mm(V("s%d" % k, 0, 256), V("idn"), z, False, False)
-            mm(V("s%d" % k, 256, 512), V("idn"), z, False, True)
-            act(V("ab", 2048 + 512 * k, 2560 + 512 * k), V("s%d" % k), Act.Abs)
-        rest = list(setup_rest()) if t == 0 else []
-        for c in range(8):
-            q = (c + t) % 8
-            tt(V("dd", 256 * c, 256 * c + 256), G(TAB(t), S("ru", t, 16 * q, 16 * q + 16)), z, Op.subtract)
-            if rest:
-                rest[c]()
-            if c % 2 and c - 1 > 8 - nrelu:
-                ts(V("ab", 256 * c - 768, 256 * c - 256), V("dd", 256 * c - 768, 256 * c - 256), 0.0, Op.max)
-        if CFG["db"]:
-            record("s", [TAB(t + 1)], [TAB(t), V("dd", 1024, 1280)], lambda a=ap(TAB(t + 1)), b=ap(TAB(t)): g.sync.dma_start(a, b),
-                   lambda p: 60.0, "m", (), lambda p: 4000.0)
-        if nrelu:
-            ts(V("ab", 1536, 2048), V("dd", 1536, 2048), 0.0, Op.max)
-        tt(VT(0), phi, plo, Op.subtract)
-
-        def low(k, stop):
-            if 4 * k >= 8 - nrelu:
-                sums("klo", 64 * k, 1024 * k, 4, "wp1", False, False, "dd")
-                sums("klo", 64 * k, 1024 * k, 4, "wn2", False, stop)
+        seen["phase"] = "l" if last else "f" if t == 0 else ""
+        kd, kf = CFG["d" if t else "d0"], CFG["flast" if last else "f"]
+        z, J, W = S("zz", t), S("jw", t, 0, 128), S("jw", t, 128, 256)
+        part = [S("pp", t, 128 * k, 128 * k + 128) for k in range(4)]
+        plo, phi = (part[0::2], part[1::2]) if t else (part[:1], part[1:2])
+        rlo, rhi = S("rs", t, 0, 128), S("rs", t, 128, 256)
+        pf, c1, a1, e1 = [S("po", t, 128 * k, 128 * k + 128) for k in range(4)]
+        J2, W2 = S("jo", t, 0, 128), S("jo", t, 128, 256)
+        for k in CFG["quads"]:
+            for c in (2 * k, 2 * k + 1):
+                sizes(kd[c], c, lambda r: rnames(t, r), z, "vv", "dd", "ab")
+        for i, k in enumerate(CFG["quads"]):
+            key, a = KEYS[i], 64 * (k % 2)
+            lin(key, [(1.0, sub(C33, 0, 64)), (-1.0, sub(J, a, a + 64)), (8.0 if k // 2 else -8.0, sub(W, a, a + 64))], True, False)
+            quad(kd, k, key, "wn64", "wp64", "ab", "dd", True)
+            if i == 0:
+                act(V("khs", 0, 64), key, Act.Copy)
+                key = V("khs", 0, 64)
             else:
-                act(V("ab", 1024 * k, 1024 * k + 512), V("dd", 1024 * k, 1024 * k + 512), Act.Abs)
-                act(V("ab", 1024 * k + 512, 1024 * k + 1024), V("dd", 1024 * k + 512, 1024 * k + 1024), Act.Abs)
-                sums("klo", 64 * k, 1024 * k, 4, "wneg", False, stop)
-        sums("khi", 0, 2048, 4, "wneg", False, False)
-        sums("khi", 64, 3072, 4, "wneg", False, False)
-        if nrelu == 8:
-            low(0, False)
-        mm(KH, V("idn"), J, False, False); mm(KH, V("idp"), Wm, False, True)
-        mm(KL, V("idn"), J, False, False); mm(KL, V("idn"), Wm, False, False)
-        mm(WmP, V("idp"), Wm, True, True)
-        if CFG["khs"] == "a" and nrelu == 8:
-            act(V("khs"), KH, Act.Copy)
-        else:
-            cp(V("khs"), KH)
-        if nrelu == 8:
-            low(1, True)
-        else:
-            low(nrelu // 4, False)
-            low(1 - nrelu // 4, True)
-        tt(V("m1", 0, 128), KL, V("khs"), Op.max)
-        tt(VT(3), V("khs"), KL, Op.subtract)
+                tt(V("m1", 64 * i - 64, 64 * i), key, V("m1", 64 * i - 128, 64 * i - 64) if i > 1 else V("khs", 0, 64), Op.max)
+            act(V("fl", 64 * k, 64 * k + 64), key, Act.Sign, LIM(1), -1.0 / 64)
         if t + 2 < ST:
-            send("ru", S("ru", t + 1), t + 2, [V("m1", 0, 128)])
+            send("ru", S("ru", t + 1), t + 2, [V("m1", 64, 128)])
         if not last:
-            send("ra", S("rs", t, 0, 128), t + 1, [V("m1", 0, 128)])
-            send("rb", S("rs", t, 128, 256), t + 1, [V("m1", 0, 128)])
-        turned(128, t, 0)
-        turned(256, t, 128)
-        tt(V("m1", 128, 192), V("m1", 0, 64), V("m1", 64, 128), Op.max)
+            send("rs", S("rs", t), t + 1, [V("m1", 64, 128)])
         tt(V("m1", 192, 224), V("m1", 128, 160), V("m1", 160, 192), Op.max)
-        tt(V("m1", 224, 240), V("m1", 192, 208), V("m1", 208, 224), Op.max)
-        tt(V("x0"), G(V("m1", 224, 240), BC), J, Op.add)
-        ts(V("sp"), V("x0"), 14, Op.arith_shift_right, 1, Op.bitwise_and)
-        ts(V("jp"), V("x0"), 14336, Op.bitwise_and)
-        tt(VT(1), V("sp"), VT(0), Op.mult)
-        tt(V("x1"), V("x0"), WmP, Op.add)
-        tt(V("pf"), plo, VT(1), Op.add)
-        tt(VT(2), phi, VT(1), Op.subtract)
-        cp(V("pu"), V("pf"))
-        tt(V("m2", 0, 128), V("pf"), V("jp"), Op.add)
-        ts(V("sr"), V("x1"), 14, Op.arith_shift_right, 1, Op.bitwise_and)
+        tt(V("mi", 0, 16), V("m1", 192, 208), V("m1", 208, 224), Op.max)
+        ts(V("mi", 16, 32), V("mi", 0, 16), 63, Op.bitwise_and)
+        tt(V("un"), G(V("mi", 16, 32), BC), J, Op.add)
+        ts(V("sp"), V("un"), M16, Op.add, M16 + 32, Op.is_equal)
+        ts(V("rr"), V("un"), M16, Op.add, M16, Op.subtract)
+        lin(DP, [(1.0, v) for v in phi] + [(-1.0, v) for v in plo])
+        lin(PL, [(1.0, v) for v in plo])
+        tt(V("t3"), V("sp"), DP, Op.mult)
+        tt(pf, V("t3"), PL, Op.add)
+        cp(V("pu"), pf)
+        lin(DLO, [(1.0, v) for v in phi] + [(-1.0, v) for v in plo] + [(-2.0, V("t3"))])
+        lin(PS, [(1.0, v) for v in phi] + [(-1.0, V("t3"))])
+        if not last:
+            send("pa", pf, t + 1)
+        lin(JP, [(1024.0, C7), (1024.0, V("un")), (-1024.0, V("rr"))])
+        tt(V("mx"), pf, JP, Op.max)
+        act(J2, JP, Act.Identity, 0.0, 1.0 / 1024)
+        if last:
+            cp(V("jp", 0, 16), sub(JP, 0, 16))
+            for k in range(3):
+                ts(V("jp", 16 * k + 16, 16 * k + 32), V("jp", 0, 16), 11 + k, Op.arith_shift_right, 1, Op.bitwise_and)
+            cp(V("tc", 0, 48), V("jp", 16, 64))
+            for k in range(3):
+                act(V("bits", 256 * k, 256 * k + 256), G(V("tc", 16 * k, 16 * k + 16), BC16), Act.Copy)
 
-        PB = ["s0", "s1", "s3"]
-
-        def pgather(k):
-            act(V("vp", 512 * k, 512 * k + 512), G(TAB(t), V("pu", 32 * k, 32 * k + 32)), Act.Copy)
-
-        def psub(k):
-            mm(V(PB[k]), V("idp"), V("vp", 512 * k, 512 * k + 512), True, False)
-            mm(V(PB[k], 0, 256), V("idn"), V("yy"), False, False)
-            mm(V(PB[k], 256, 512), V("idn"), V("yy"), False, True)
-        right = [lambda: ts(V("thr"), V("jp"), 2048.0, Op.not_equal, LIM(0), Op.mult),
-                 lambda: tt(V("tq"), V("sr"), VT(3), Op.mult),
-                 lambda: tt(V("t2"), V("sr"), dR, Op.mult),
-                 lambda: tt(VT(3), V("tq"), KL, Op.add),
-                 lambda: tt(V("rf"), V("t2"), rlo, Op.add),
-                 lambda: tt(VT(0), V("thr"), VT(3), Op.is_gt)]
-
-        def filler(on=True):
-            if right and on:
-                right.pop(0)()
-        early = min(npa // 2, CFG["early"])
-        for k in range(early):
-            pgather(k)
-        tt(V("m2", 128, 192), V("m2", 0, 64), V("m2", 64, 128), Op.min)
-        filler(CFG["fill"] > 0)
-        tt(V("m2", 192, 224), V("m2", 128, 160), V("m2", 160, 192), Op.min)
-        filler(CFG["fill"] > 1)
-        tt(V("m2", 224, 240), V("m2", 192, 208), V("m2", 208, 224), Op.min)
-        filler(CFG["fill"] > 2)
-        cp(V("yu"), V("m2", 224, 240))
-        filler(CFG["fill"] > 3)
+        def ysum():
+            for q in range(8):
+                r = g.tensor.matmul(ap(YS), ap(ID(1.0)), ap(V("mx", 16 * q, 16 * q + 16)), q == 0, q == 7)
+            return r
+        record("t", [YS], [ID(1.0), V("mx")], ysum, lambda p: 512 * p["pe"])
+        ts(V("yu"), YS, -28.0 * 2048, Op.add)
+        for c in range(4):
+            if kf[c] in "ab":
+                (cp if kf[c] == "b" else lambda o, a: act(o, a, Act.Copy))(
+                    V("vp", 512 * c, 512 * c + 512), G(TAB, V("pu", 32 * c, 32 * c + 32)))
         if CFG["y"] == "v":
-            cp(V("yy"), G(TAB(t), V("yu")))
-            mm(V("msc", 256, 512), V("idp"), V("yy"), True, False); mm(V("msc", 256, 512), V("idn"), z, False, True)
-            act(S("zo", t), V("msc", 256, 512), Act.Abs)
+            cp(V("yy"), G(TAB, V("yu")))
+            lin(DZ, [(1.0, V("yy")), (-1.0, z)])
+            act(S("zo", t), DZ, Act.Abs)
         else:
-            tt(V("dz"), G(TAB(t), V("yu")), z, Op.subtract)
-            act(V("yy"), G(TAB(t), V("yu")), Act.Copy)
+            tt(V("dz"), G(TAB, V("yu")), z, Op.subtract)
+            act(V("yy"), G(TAB, V("yu")), Act.Copy)
             act(S("zo", t), V("dz"), Act.Abs)
         if not last:
             send("zz", S("zo", t), t + 1)
         else:
             store("s", T.yz[:], ap(S("zo", t)), S("zo", t))
-        sums("khi", 384, 0, 1, "wpos", True, True, "yy")
-        for k in range(early, npa // 2):
-            pgather(k)
-        if CFG["avg"] == "a" or last:
-            mm(V("msc", 0, 256), V("idp"), V("yy"), True, False); mm(V("msc", 0, 256), V("idp"), z, False, True)
-            act(V("hm"), V("msc", 0, 256), Act.Identity, MAGIC, 0.5 - 2.0 ** -11)
-            act(V("avg"), V("hm"), Act.Identity, -MAGIC)
-        else:
-            mm(V("msc", 0, 256), V("idh"), V("qtr"), True, False)
-            mm(V("msc", 0, 256), V("idh"), V("yy"), False, False); mm(V("msc", 0, 256), V("idh"), z, False, True)
-        for k in range(npa // 2):
-            psub(k)
-            act(V("abp", 512 * k, 512 * k + 512), V(PB[k]), Act.Abs)
-        cp(V("ui", 0, 16), V("khi", 384, 400))
-        ts(V("ui", 16, 32), V("ui", 0, 16), 7, Op.bitwise_and)
-        tt(V("ui", 32, 48), V("ui", 16, 32), V("base"), Op.add)
-        cp(V("uu"), V("ui", 32, 48))
-        if CFG["avg"] == "v" and not last:
-            ts(V("avg"), V("msc", 0, 256), MAGIC, Op.add, MAGIC, Op.subtract)
-        for c in range(npa, 8):
-            tt(V("dp", 256 * c, 256 * c + 256), G(TAB(t), V("pu", 16 * c, 16 * c + 16)), V("yy"), Op.subtract)
-            if c == 7 and CFG["prelu"]:
-                ts(V("abp", 1536, 2048), V("dp", 1536, 2048), 0.0, Op.max, 2.0, Op.mult)
-            elif c % 2:
-                act(V("abp", 256 * c - 256, 256 * c + 256), V("dp", 256 * c - 256, 256 * c + 256), Act.Abs)
-        for k in CFG["ford"]:
-            if k and CFG["prelu"]:
-                sums("khi", 224, 1536, 2, "wm1", True, False, "dp")
-            sums("khi", 128 + 64 * k, 1024 * k, 4, "wpos", not (k and CFG["prelu"]), True, "abp")
-        cp(G(TAB(t + 1), V("uu")), V("avg"))
-        if last:
-            store("s", T.yx[:], ap(TAB(t + 1)), TAB(t + 1), 6000.0)
-        else:
-            pregather(t + 1, 0)
-        act(V("sg"), FF, Act.Sign, LIM(1))
-        act(EE, V("sg"), Act.Relu, acc=V("cnt", 0, 1))
-        while right:
-            filler()
-        tt(V("prod"), G(V("rf"), SH1), V("pf"), Op.mult)
-        tt(V("wn"), V("sr"), VT(0), Op.not_equal)
-        ts(V("pa"), V("prod"), LIM(2), Op.add)
+        lin(UU, [(1.0, M35)], True, False)
+        sums(UU, "wp1", "yy", 0, 1, False, True)
+        ts(V("r8", 0, 16), UU, M8, Op.add, M8, Op.subtract)
+        tt(V("r8", 16, 32), UU, V("r8", 0, 16), Op.subtract)
+        lin(UU, [(1.0, V("r8", 16, 32)), (1.0, V("b16"))])
+        ts(V("uu"), UU, 3.5, Op.add)
+        lin(AVG, [(1.0, V("yy")), (1.0, z)])
+        ts(V("avg"), AVG, 0.5 - 2.0 ** -11, Op.mult)
+        lin(X, [(1.0, V("un"), 16), (-8.0, W, 16)])
+        act(V("ww"), X, Act.Abs, -26.0)
+        ts(V("sr"), V("ww"), M16, Op.add, M16 + 16, Op.is_equal)
+        turn = 16 * (t + 1)
+        lin(DR, [(1.0, rhi, turn), (-1.0, rlo, turn)])
+        lin(AB, [(1.0, V("fl", 0, 128), 16), (1.0, V("fl", 128, 256), 16)])
+        tt(V("t2"), V("sr"), DR, Op.mult)
+        tt(V("s1"), V("sr"), AB, Op.mult)
+        lin(RF, [(1.0, C32), (1.0, rlo, turn), (1.0, V("t2"))])
+        lin(S2, [(1.0, C1), (1.0, V("fl", 0, 128), 16), (-2.0, V("sr")), (-1.0, V("s1"))])
+        tt(V("s3"), J2, S2, Op.mult)
+        lin(WX, [(1.0, V("s3")), (1.0, V("sr"))])
+        act(W2, WX, Act.Sign, -0.5)
         if not last:
-            cp(S("jo", t, 0, 128), V("jp"))
-            act(S("jo", t, 128, 256), G(V("wn"), SH1), Act.Identity, -2048.0, 16384.0)
             send("jw", S("jo", t), t + 1)
-            mm(V("msc", 272, 273), V("blk"), V("cnt", 0, 1), True, True)
-            pregather(t + 1, 1, False)
-        tt(V("dlo"), VT(2), V("pf"), Op.subtract)
+        if t:
+            tt(V("prod"), pf, RF, Op.mult)
+            ts(V("pa"), V("prod"), LIM(2), Op.add)
+        else:
+            tt(V("pa"), pf, RF, Op.mult)
         ts(V("new"), V("pa"), 5, Op.arith_shift_right, 2047, Op.bitwise_and)
-        tt(VT(1), V("dlo"), EE, Op.mult)
-        tt(V("dhi"), V("new"), VT(2), Op.subtract)
-        tt(S("po", t, 0, 128), V("pf"), VT(1), Op.add)
-        tt(V("ahi"), V("dhi"), EE, Op.mult)
-        if not last:
-            cp(V("ai", 0, 1), V("msc", 272, 273))
-        tt(S("po", t, 128, 256), V("ahi"), VT(2), Op.add)
-        if not last:
-            send("pa", S("po", t, 0, 128), t + 1)
-            send("pb", S("po", t, 128, 256), t + 1)
-            ts(V("ai", 1, 2), V("ai", 0, 1), 31, Op.bitwise_and)
-            ts(LIM(2), V("ai", 0, 1), 32.0, Op.mult)
-            pregather(t + 1, 2, False)
-            limits()
-            pregather(t + 1, 3, False)
+        if last:
+            tt(V("t2"), W2, DR, Op.mult)
+            for h in range(2):
+                lin(V("pklo", 128 * h, 128 * h + 128), [(-0.5 if h else 0.5, V("t2")), (0.5, rlo, turn), (0.5, rhi, turn)])
+            cp(V("xr", 0, 256), V("pklo", 0, 256))
+            in_order("xr", ("pb6", "pklo", "pb6", "pklo"), "ta", "orr", T.yr, "s")
+        for c in range(4):
+            sizes(kf[c], c, lambda r: V("pu", 16 * r, 16 * r + 16), V("yy"), "vp", "dp", "abp")
+        cp(G(TAB, V("uu")), V("avg"))
+        if last:
+            store("s", T.yx[:], ap(TAB), TAB, 5000.0)
+        else:
+            ahead(t + 1, CFG["d"])
+        lin(FF, [(1.0, C0)], True, False)
+        for k in range(2):
+            quad(kf, k, sub(FF, 64 * k, 64 * k + 64), "wp1", "wn1", "abp", "dp", k == 1)
+        if CFG["e"] == "v":
+            ts(V("ee"), FF, LIM(1), Op.add, 0.0, Op.is_gt)
+        else:
+            act(V("sg"), FF, Act.Sign, LIM(1))
+            act(V("ee"), V("sg"), Act.Relu)
+        act(V("eb"), V("ee"), Act.Identity, 1.0, -1.0, None if last else V("cnt", 0, 1))
+        lin(EP, [(1.0, V("ee"))])
+        if last:
+            tt(V("pb7", 0, 128), V("ee"), DLO, Op.mult)
+            tt(c1, V("eb"), PS, Op.mult)
+            tt(V("pb7", 128, 256), V("new"), EP, Op.mult)
+            tt(V("xp", 0, 128), pf, V("pb7", 0, 128), Op.add)
+            tt(V("xp", 128, 256), c1, V("pb7", 128, 256), Op.add)
+        else:
+            tt(a1, V("ee"), DLO, Op.mult)
+            tt(c1, V("eb"), PS, Op.mult)
+            tt(e1, V("new"), EP, Op.mult)
+            send("pb", S("po", t, 128, 512), t + 1)
+            mm(CNT, V("blk"), V("cnt", 0, 1), True, True)
+            act(LIM(2), CNT, Act.Copy)
+            cp(V("ai", 0, 1), LIM(2))
+            ts(V("ai", 1, 2), V("ai", 0, 1), 5, Op.arith_shift_right, 31, Op.bitwise_and)
+            ts(LIM(1), V("ai", 1, 2), -1.0, Op.mult, LIM(0), Op.add)
 
     seen.clear()
-    seen.update({q + k: 50 for q in "vat" for k in SCRATCH})
-    ts(V("coli", 4, 5), V("coli", 1, 2), 1, Op.arith_shift_right)
-    ts(V("coli", 5, 6), V("coli", 1, 2), 2, Op.arith_shift_right)
-    cp(C(8), V("coli", 4, 5)); cp(C(9), V("coli", 5, 6))
-    ts(B2, V("li", 72, 80), C(8), Op.add); ts(B3, V("li", 80, 88), C(9), Op.add)
-    ts(C(7), V("coli", 3, 4), 15.0, Op.mult, C(0), Op.add)
-    ts(INV1, V("li", 136, 152), C(7), Op.add)
-    act(V("td"), G(S("po", ST - 1), P1), Act.Identity, -32.0, 2048.0)
-    tt(V("t2"), V("wn"), dR, Op.mult)
-    act(V("tq"), dR, Act.Copy)
-    tt(V("ta", 0, 128), V("t2"), rlo, Op.add)
-    tt(VT(0), V("tq"), rlo, Op.add)
-    tt(V("ta", 128, 256), VT(0), V("t2"), Op.subtract)
-    for k, lst in enumerate((B1, B2, B3)):
-        ts(V("bits", 128 * k, 128 * k + 128), G(V("jp"), lst), 13 - k, Op.arith_shift_right, 1, Op.bitwise_and)
-    tt(V("tb"), G(V("ta"), PK), V("td"), Op.add)
-    cur, oth = "tb", "ta"
-    for k in range(3):
-        tt(VT(0), V(cur, 128, 256), V(cur, 0, 128), Op.subtract)
-        tt(VT(1), V("bits", 128 * k, 128 * k + 128), VT(0), Op.mult)
-        tt(V(oth, 0, 256, 2), V(cur, 0, 128), VT(1), Op.add)
-        tt(V(oth, 1, 256, 2), V(cur, 128, 256), VT(1), Op.subtract)
-        cur, oth = oth, cur
-    cp(V(oth), G(V(cur), INV1))
-    tr(V(cur), V(oth))
-    cp(V("ti"), G(V(cur), INV2))
-    act(V("td"), G(V(cur), INV2), Act.Identity, 2.0 ** -12 - 0.5, 2.0 ** -11)
-    ts(V("tj"), V("ti"), 2047, Op.bitwise_and)
-    act(V("te"), V("td"), Act.Identity, MAGIC)
-    cp(V("orr"), V("tj"))
-    act(V("op"), V("te"), Act.Identity, -MAGIC)
-    for (sp_, sc_, dp_, dc_) in blocks():
-        store("s", T.yr[dp_, dc_], T.orr[sp_, sc_], V("orr"))
-    for (sp_, sc_, dp_, dc_) in blocks():
-        store("a", T.yp[dp_, dc_], T.op[sp_, sc_], V("op"))
+    seen["phase"] = "z"
+    in_order("xp", ("ps0", "ps2", "pb6", "pklo"), "tb", "op", T.yp, "sa")
     emit()
     g.sync.wait_ge(T.sem.sto, cnt["sto"])
-    for s in ("sent", "cv", "ca", "ct", "cg") + (("cpy",) if CFG["db"] else ()):
+    for s in ("sent", "cv", "ca", "ct", "cg"):
         g.wait_ge(T.sem[s], cnt[s])

import numpy as np
from concourse.mybir import AluOpType as Op, ActivationFunctionType as Act

ST = 6
MAGIC = float(3 * 2 ** 22)
M8, M16 = 8 * MAGIC, 16 * MAGIC
F, H, I, U, S16 = "float32", "bfloat16", "int32", "uint16", "float16"


def _sb(n, d):
    return ("sbuf", [128, n], d)


SCRATCH = {
    "tab": _sb(2048, H), "vv": _sb(4096, H), "dd": _sb(4096, H), "ab": _sb(4096, H),
    "vp": _sb(2048, H), "dp": _sb(2048, H), "abp": _sb(2048, H),
    "zz": _sb(256 * ST, H), "zo": _sb(256 * ST, H), "jw": _sb(256 * ST, H), "jo": _sb(256 * ST, H),
    "pp": _sb(512 * ST, S16), "po": _sb(512 * ST, S16), "ru": _sb(256 * ST, U), "rs": _sb(256 * ST, S16),
    "pin": _sb(256, I), "rin": _sb(256, I), "thi": _sb(4, I), "ta": _sb(256, F), "tb": _sb(256, F), "tc": _sb(256, F),
    "td": _sb(256, F), "te": _sb(256, F), "ti": _sb(256, I), "tj": _sb(256, I), "op": _sb(256, F), "orr": _sb(256, F),
    "col": _sb(16, F), "coli": _sb(8, I), "cidx": _sb(144, F), "blk": _sb(128, F), "blki": _sb(128, F),
    "wn64": _sb(144, H), "wp64": _sb(144, H), "wp1": _sb(144, H), "wn1": _sb(144, H), "ids": _sb(128 * 9, H),
    "cst": _sb(128 * 5 + 256 + 16, H), "li": _sb(160, I), "lu": _sb(160, U), "base": _sb(16, I), "b16": _sb(16, S16), "q2": _sb(128, I),
    "khs": _sb(128, F), "m1": _sb(256, F), "mi": _sb(32, I), "un": _sb(128, H), "sp": _sb(128, H), "rr": _sb(128, H),
    "t3": _sb(128, S16), "pu": _sb(128, U), "mx": _sb(128, S16), "yu": _sb(16, U), "yy": _sb(256, H), "dz": _sb(256, H),
    "avg": _sb(256, I), "r8": _sb(32, S16), "uu": _sb(16, U), "fl": _sb(256, H), "ww": _sb(128, H), "sr": _sb(128, H),
    "t2": _sb(128, S16), "s1": _sb(128, H), "s3": _sb(128, H), "prod": _sb(128, F), "pa": _sb(128, I), "new": _sb(128, I),
    "sg": _sb(128, H), "ee": _sb(128, H), "eb": _sb(128, H), "cnt": _sb(4, F), "ai": _sb(8, I), "lim": _sb(16, F),
    "jp": _sb(64, I), "bits": _sb(768, H), "xp": _sb(1024, S16), "xr": _sb(1024, S16),
}
for _b in ("s0", "s2", "s4", "klo", "khi", "b5", "b6", "b7"):
    SCRATCH["p" + _b] = ("psum", [128, 512], F)
STAGE = ["ps0", "ps2"]
IDS = [1.0, -1.0, 0.5, -0.5, 8.0, -8.0, 1024.0, -1024.0, -2.0]
STREAMS = {"ru": ("ru", 256, 0, 256), "rs": ("rs", 256, 0, 256), "pa": ("pp", 512, 0, 128), "zz": ("zz", 256, 0, 256),
           "jw": ("jw", 256, 0, 256), "pb": ("pp", 512, 128, 512)}
CFG = {"d": "vvvmaaaa", "f": "aamv", "flast": "aaam", "d0": "vvvvaaaa", "e": "v", "y": "v", "quads": (0, 2, 3, 1)}
PAR = {"c": 1.0, "g": 1.5, "scat": 3.8, "fix": 30.0, "pe": 0.5, "wake": 100.0, "issue": 400.0, "hop": 3400.0, "w": 2 / 120}
PARS = [PAR, dict(PAR, g=1.04, scat=1.6, wake=50.0, hop=3000.0, w=1 / 100),
        dict(PAR, g=2.08, scat=6.0, wake=200.0, pe=0.63, hop=5500.0, w=1 / 160)]
TRIES = [300, 1, 1.0, 22000]
PLAN = {}
ORDER = [("ru", 1)] + [x for t in range(1, ST) for x in (
    ("ru", t + 1), ("rs", t), ("pa", t), ("zz", t), ("jw", t), ("pb", t)) if x[1] < ST]


def relay_of(s, t):
    return {"ru": 2 * (1 - t % 2), "zz": 0, "rs": 1 + 2 * (t % 2), "jw": 3, "pa": 1, "pb": 2}[s]


SEMAPHORES = (["cv", "ca", "ct", "cg", "ldr", "ldx", "ldz", "ldp", "sto", "sent"]
              + ["a%s%d" % (s, t) for s in STREAMS for t in range(1, ST)])


def relays(T, topo, rank):
    src, dst = T.cores[rank], T.cores[(rank + 1) % len(T.cores)]
    if topo.may_write(src, dst):
        return []
    c = [x for x in topo.cores_of(src) if T.rank_of(x) is None and topo.may_write(x, dst)]
    return sorted(c, key=lambda x: topo.die(x) != topo.die(src))


def slot(T, s, t):
    name, w, a, b = STREAMS[s]
    return T[name][:, w * t + a:w * t + b]


def relay_program(g, core, T, topo):
    n = len(T.cores)
    for r in range(n):
        rl = relays(T, topo, r)
        if core not in rl:
            continue
        src, dst = T.cores[r], T.cores[(r + 1) % n]
        got, m = len(topo.engines(src, core)), topo.mask(core, dst)
        rid, pid = topo.addr(dst, core)
        sent = 0
        for s, t in ORDER:
            if rl[relay_of(s, t)] == core:
                sem = T.sem["a%s%d" % (s, t)]
                g.wait_ge(sem, got)
                g.remote_dma(slot(T, s, t), slot(T, s, t), sem, T.sem.sent, pid, rid, m)
                sent += len(topo.engines(core, dst))
        g.wait_ge(T.sem.sent, sent)


def improve(ops, order, tries):
    m, rng, K = len(ops), np.random.RandomState(0), range(len(PARS))
    qs = [o["q"] for o in ops]
    pre = [[[(j, ops[j]["ls"][k] + PARS[k]["wake"]) for j in o["wait"]]
            + [(j, ops[j]["ls"][k]) for j in o["order"] if o["q"] == "x"] for o in ops] for k in K]
    dep = [set(o["wait"]) | set(o["order"]) for o in ops]
    same = {}
    for i, o in enumerate(ops):
        same.setdefault(o["id"], []).append(i)

    def times(od, k):
        end, free, why, pk, top = [0.0] * m, {}, [-1] * m, pre[k], (0.0, 0)
        for i in od:
            t0, w = free.get(qs[i], (0.0, -1))
            for j, d in pk[i]:
                if end[j] + d >= t0:
                    t0, w = end[j] + d, j
            end[i], why[i] = t0 + ops[i]["cs"][k], w
            if qs[i] != "x":
                free[qs[i]] = (end[i], i)
            if end[i] + ops[i]["ls"][k] > top[0]:
                top = (end[i] + ops[i]["ls"][k], i)
        return top[0], why, top[1]

    def score(od):
        r = [times(od, k) for k in K]
        return sum(r[k][0] * PARS[k]["w"] for k in K), r

    def move(od, i, j):
        a, b = od.index(j), od.index(i)
        need, queues, first = {i}, set(), []
        for x in reversed(od[a:b + 1]):
            if x in need or qs[x] in queues:
                if x == j:
                    return od
                first.append(x)
                need |= dep[x]
                if qs[x] != "x" and x != i:
                    queues.add(qs[x])
        fs = set(first)
        return od[:a] + first[::-1] + [x for x in od[a:b + 1] if x not in fs] + od[b + 1:] if a < b else od

    now = best = score(order)
    cur = order
    for n in range(tries):
        _, why, i = now[1][rng.randint(len(PARS))]
        pairs = []
        while why[i] >= 0:
            if qs[why[i]] == qs[i] and why[i] not in dep[i]:
                pairs.append((i, why[i]))
            i = why[i]
        if not pairs:
            break
        i, j = pairs[rng.randint(len(pairs))]
        u = rng.rand()
        if u < 0.5:
            qq = [x for x in cur if qs[x] == qs[i]]
            k = qq.index(j)
            if u < 0.25:
                j = qq[max(0, k - rng.randint(4))]
            else:
                i = qq[min(len(qq) - 1, k + 1 + rng.randint(4))]
        todo = [(i, j)]
        if rng.rand() < 0.6:
            si, sj = same[ops[i]["id"]], same[ops[j]["id"]]
            d = si.index(i) - sj.index(j)
            todo = [(si[k], sj[k - d]) for k in range(len(si)) if 0 <= k - d < len(sj)]
        od = cur
        for a, b in todo:
            od = move(od, a, b)
        if od is not cur:
            x = score(od)
            if x[0] <= now[0] + 5.0 * (1 - n / tries) * rng.exponential():
                cur, now = od, x
                if x[0] < best[0]:
                    best, order = x, od
    return order, (best[0], [r[0] for r in best[1]])


def rank_program(g, core, T, topo):
    rank = T.rank_of(core)
    if rank is None:
        return relay_program(g, core, T, topo)
    n = len(T.cores)
    nxt, prv = T.cores[(rank + 1) % n], T.cores[(rank - 1) % n]
    rl_out, rl_in = relays(T, topo, rank), relays(T, topo, (rank - 1) % n)

    Q = {"v": g.vector, "a": g.scalar, "t": g.tensor, "g": g, "s": g.sync}
    SEM = {"v": "cv", "a": "ca", "t": "ct", "g": "cg"}
    cnt = {"cv": 0, "ca": 0, "ct": 0, "cg": 0, "sent": 0, "sto": 0}
    known = {q: {} for q in Q}
    hist = {}
    psum = [k for k in SCRATCH if SCRATCH[k][0] == "psum"]

    def V(name, a=0, b=None, step=1):
        return (name, a, SCRATCH[name][1][1] if b is None else b, step)

    def sub(v, a, b):
        return (v[0], v[1] + a, v[1] + b, 1)

    def G(win, off):
        return ("ind", win, off)

    def ap(v):
        if v[0] == "ind":
            return ap(v[1]).indirect(ap(v[2]))
        return T[v[0]][:, v[1]:v[2]] if v[3] == 1 else T[v[0]][:, v[1]:v[2]:v[3]]

    def arg(v):
        return ap(v) if isinstance(v, tuple) else v

    ops, sends, banks, seen = [], {}, {}, {}

    def size(v):
        return 16 * (v[2][2] - v[2][1]) if v[0] == "ind" else len(range(v[1], v[2], v[3]))

    def cost(q, outs, ins, PAR):
        o, m = outs[0], size(outs[0])
        vs = [v for v in ins if isinstance(v, tuple)]
        if q == "t":
            return max(64, m) * PAR["pe"] * (4 if SCRATCH[vs[0][0]][2] == F else 1)
        if q == "g":
            return 130 + 2 * m * PAR["c"]
        if o[0] == "ind":
            return 50 + m * PAR["scat"] * PAR["c"]
        if any(v[0] == "ind" for v in vs):
            return 55 + m * PAR["g"] * PAR["c"]
        full = [v for v in vs if size(v) == m]
        per = 1.0
        if q == "v" and len(full) == 2:
            per = 1.0 if any(v[0] in psum for v in full) else 2.0
        elif q == "v" and all(SCRATCH[v[0]][2] in (H, U, S16) for v in full + [o]):
            per = 0.5
        return PAR["fix"] + max(64, m * per) * PAR["c"]

    def split(outs, ins):
        wr, rd = [], []
        for v in outs:
            if v[0] == "ind":
                wr.append(v[1]); rd.append(v[2])
            else:
                wr.append(v)
        for v in ins:
            if isinstance(v, tuple):
                if v[0] == "ind":
                    rd.append(v[1]); rd.append(v[2])
                else:
                    rd.append(v)
        return wr, rd

    def record(q, wr, rd, call, c, kind="c", order=(), lat=None, tok=None):
        wait, order, me = set(), set(order), len(ops)
        for kd, vs in (("w", wr), ("r", rd)):
            for v in vs:
                for (a, b, k2, q2, i) in hist.get(v[0], []):
                    if v[3] == 2 and v[1] == a + 1 and k2 == "w" and i == me - 1:
                        continue
                    if not (q == "t" and q2 == "t") and a < v[2] and v[1] < b and (kd == "w" or k2 == "w"):
                        wait.add(i)
        for name in set(v[0] for v in wr + rd if v[0] in psum):
            bk = banks.setdefault(name, {"q": q, "now": [], "was": [], "pe": []})
            if bk["q"] != q:
                bk.update(q=q, was=bk["now"], now=[])
            wait.update(bk["was"])
            bk["now"].append(me)
            if q == "t":
                order.update(bk["pe"])
                bk["pe"] = [me]
        name = q + (wr[0][0] if wr else rd[0][0])
        seen[name] = seen.get(name, 0) + 1
        ops.append({"id": "%s%s%d" % (seen.get("phase", ""), name, seen[name]), "q": q, "call": call, "cs": [c(p) for p in PARS],
                    "ls": [lat(p) for p in PARS] if lat else [0.0] * len(PARS), "c": c(PAR), "lat": lat(PAR) if lat else 0.0,
                    "kind": kind, "wait": sorted(wait), "order": sorted(order), "tok": tok})
        for v in wr:
            hist[v[0]] = [e for e in hist.get(v[0], []) if not (v[1] <= e[0] and e[1] <= v[2])] + [(v[1], v[2], "w", q, me)]
        for v in rd if kind == "c" else []:
            hist[v[0]] = hist.get(v[0], []) + [(v[1], v[2], "r", q, me)]
        return me

    def run(q, outs, ins, call):
        wr, rd = split(outs, ins)
        record(q, wr, rd, call, lambda p: cost(q, outs, ins, p))

    def length(order):
        total = []
        for k, p in enumerate(PARS):
            free, fin = {}, [0.0] * len(ops)
            for i in order:
                o = ops[i]
                t0 = free.get(o["q"], 0.0)
                for j in o["wait"]:
                    if fin[j] + p["wake"] > t0:
                        t0 = fin[j] + p["wake"]
                if o["q"] == "x":
                    t0 = max([t0] + [fin[j] for j in o["order"]])
                else:
                    free[o["q"]] = t0 + o["cs"][k]
                fin[i] = t0 + o["cs"][k] + o["ls"][k]
            total.append(max(fin))
        return sum(x * p["w"] for x, p in zip(total, PARS)), total

    def best_plan():
        rng = np.random.RandomState(TRIES[1])
        ids = sorted(o["id"] for o in ops if o["q"] in "vatg")
        boost = {}
        order = plan(boost)
        best = now = length(order)
        for it in range(TRIES[0]):
            b = dict(boost)
            for _ in range(1 + int(rng.randint(3))):
                k = ids[rng.randint(len(ids))]
                u = rng.rand()
                b[k] = 0 if u < 0.2 else max(-1000, b.get(k, 0) + 100 * int(rng.randn() * (4 if u < 0.6 else 20)))
            od = plan(b)
            x = length(od)
            if x[0] <= now[0] + TRIES[2] * (1.0 - it / TRIES[0]) * rng.exponential():
                boost, now = b, x
                if x[0] <= best[0]:
                    order, best = od, x
        order, best = improve(ops, order, TRIES[3])
        PLAN.update(length=best, ops=ops)
        return order

    def plan(boost):
        m = len(ops)
        up = [0.0] * m
        for i in range(m - 1, -1, -1):
            up[i] += max(1.0, ops[i]["c"] + boost.get(ops[i]["id"], 0)) + ops[i]["lat"]
            for j in ops[i]["wait"]:
                up[j] = max(up[j], up[i] + PAR["wake"])
            for j in ops[i]["order"]:
                up[j] = max(up[j], up[i] - (0.0 if ops[i]["q"] == "x" else ops[j]["lat"]))
        start, busy = [0.0] * m, {q: [] for q in Q}
        for i in sorted(range(m), key=lambda i: (-up[i], i)):
            o = ops[i]
            t0 = max([start[j] + ops[j]["c"] + ops[j]["lat"] + PAR["wake"] for j in o["wait"]]
                     + [start[j] + ops[j]["c"] + (ops[j]["lat"] if o["q"] == "x" else 0.001) for j in o["order"]] + [0.0])
            if o["q"] != "x":
                b = busy[o["q"]]
                k = bisect(b, t0)
                while k < len(b) and b[k][0] < t0 + o["c"]:
                    t0 = max(t0, b[k][1])
                    k += 1
                b.insert(k, (t0, t0 + o["c"]))
            start[i] = t0
        return sorted(range(m), key=lambda i: (start[i], i))

    def bisect(b, t0):
        lo, hi = 0, len(b)
        while lo < hi:
            mid = (lo + hi) // 2
            if b[mid][1] <= t0:
                lo = mid + 1
            else:
                hi = mid
        return lo

    def emit():
        if "order" not in PLAN:
            PLAN["order"] = best_plan()
        for i in PLAN["order"]:
            o = ops[i]
            q = o["q"]
            if q == "x":
                continue
            toks, k = {}, known[q]
            for j in o["wait"]:
                tk = ops[j]["tok"]
                if tk[0] not in toks or toks[tk[0]][1] < tk[1]:
                    toks[tk[0]] = tk
            for sem, val, clock in sorted(toks.values(), key=lambda tk: tk[0] == SEM.get(q)):
                if k.get(sem, 0) < val:
                    Q[q].wait_ge(T.sem[sem], val)
                    k[sem] = val
                    for s in clock:
                        k[s] = max(k.get(s, 0), clock[s])
            if o["kind"] == "c":
                cnt[SEM[q]] += 1
                o["call"]().then_inc(T.sem[SEM[q]], 1)
                o["tok"] = (SEM[q], cnt[SEM[q]], dict(k))
            else:
                o["call"]()

    def tt(o, a, b, op):
        run("v", [o], [a, b], lambda: g.vector.tensor_tensor(ap(o), ap(a), ap(b), op))

    def ts(o, a, s1, op0, s2=None, op1=None):
        if op1 is None:
            run("v", [o], [a, s1], lambda: g.vector.tensor_scalar(ap(o), ap(a), arg(s1), None, op0))
        else:
            run("v", [o], [a, s1, s2], lambda: g.vector.tensor_scalar(ap(o), ap(a), arg(s1), arg(s2), op0, op1))

    def cp(o, a):
        run("v", [o], [a], lambda: g.vector.tensor_copy(ap(o), ap(a)))

    def ms(o, c):
        run("v", [o], [], lambda: g.vector.memset(ap(o), c))

    def tr(o, a):
        run("v", [o], [a], lambda: g.vector.transpose(ap(o), ap(a)))

    def act(o, a, f, bias=0.0, scale=1.0, acc=None):
        if acc is None:
            run("a", [o], [a, bias, scale], lambda: g.scalar.activation(ap(o), ap(a), f, bias=arg(bias), scale=arg(scale)))
        else:
            run("a", [o, acc], [a, bias, scale],
                lambda: g.scalar.activation(ap(o), ap(a), f, bias=arg(bias), scale=arg(scale), accum_out=ap(acc)))

    def mm(o, w, x, start, stop):
        run("t", [o], [w, x], lambda: g.tensor.matmul(ap(o), ap(w), ap(x), start, stop))

    def ID(x):
        k = IDS.index(x)
        return V("ids", 128 * k, 128 * k + 128)

    def lin(o, terms, start=True, stop=True):
        m = o[2] - o[1]
        terms = [(x[0], x[1], x[2] % m if len(x) > 2 else 0) for x in terms]
        terms.sort(key=lambda x: x[2] > 0)
        if terms[0][2] == 0 or not start:
            groups = [[(x, y, a, b, (a + r) % m) for x, y, r in terms for a, b in ((0, m - r), (m - r, m)) if a < b]]
        else:
            cuts = sorted(set([0, m] + [m - r for _, _, r in terms]))
            groups = [[(x, y, a, b, (a + r) % m) for x, y, r in terms] for a, b in zip(cuts, cuts[1:])]

        def call():
            for gr in groups:
                for k, (x, y, a, b, c) in enumerate(gr):
                    last = g.tensor.matmul(ap(sub(o, a, b)), ap(ID(x)), ap(sub(y, c, c + b - a)), start and k == 0, stop and k == len(gr) - 1)
            return last
        record("t", [o], [ID(x) for x in set(x[0] for x in terms)] + [x[1] for x in terms], call,
               lambda p: sum(max(64, e[3] - e[2]) for gr in groups for e in gr) * p["pe"])

    def iota(o, pat, base=0, cm=0):
        if SCRATCH[o[0]][2] == I:
            run("g", [o], [], lambda: g.iota(ap(o), pat, base, cm))
        else:
            run("g", [o], [], lambda: g.iota(ap(o), pat, base, cm, allow_small_or_imprecise_dtypes=True))

    def landed(v, sem, val, at, order=()):
        record("x", [v], [], None, lambda p: 0.0, "x", order, lambda p: at, (sem, val, {}))

    def send(s, src, t, after=()):
        to = rl_out[relay_of(s, t)] if rl_out else nxt
        rid, pid = topo.addr(to, core)
        cnt["sent"] += len(topo.engines(core, to))
        me = record("g", [], [src] + list(after), lambda: g.remote_dma(
            slot(T, s, t), ap(src), T.sem["a%s%d" % (s, t)], T.sem.sent, pid, rid, topo.mask(core, to)),
            lambda p: p["issue"], "r", [sends["last"]] if sends else [], lambda p: p["hop"] + (600.0 if s == "pb" else 0.0))
        assert ORDER[sends.get("n", 0)] == (s, t)
        sends.update(last=me, n=sends.get("n", 0) + 1)
        name, w, a, b = STREAMS[s]
        landed(V(name, w * t + a, w * t + b), "a%s%d" % (s, t), len(topo.engines(rl_in[relay_of(s, t)] if rl_in else prv, core)), 0.0, [me])

    def store(q, dst, src, v, lat=2200.0):
        cnt["sto"] += 16
        record(q, [], [v], lambda: Q[q].dma_start(dst, src).then_inc(T.sem.sto, 16), lambda p: 100.0, "d", (), lambda p: lat)


    def blocks():
        for gg in range(4):
            for x in range(2):
                yield slice(32 * gg, 32 * gg + 32), slice(128 * x, 128 * x + 128), slice(32 * gg + 16 * x, 32 * gg + 16 * x + 16)

    def S(name, t, a=0, b=None):
        w = SCRATCH[name][1][1] // ST
        return V(name, w * t + a, w * t + (w if b is None else b))

    for k, (sp_, sc_, rows) in enumerate(blocks()):
        Q["sa"[k % 2]].dma_start(T.rin[sp_, sc_], T.pr[rows, :]).then_inc(T.sem.ldr, 16)
    g.sync.dma_start(T.tab[:], T.xt[:]).then_inc(T.sem.ldx, 16)
    g.scalar.dma_start(T.zz[:, 0:256], T.z0[:]).then_inc(T.sem.ldz, 16)
    g.scalar.dma_start(T.thi[:, 0:1], T.th[:], ).then_inc(T.sem.ldz, 16)
    for (sp_, sc_, rows) in blocks():
        g.sync.dma_start(T.pin[sp_, sc_], T.pl[rows, :]).then_inc(T.sem.ldp, 16)
    landed(V("rin"), "ldr", 128, 2500.0); landed(V("tab"), "ldx", 16, 4300.0); landed(S("zz", 0), "ldz", 32, 4300.0)
    landed(V("thi"), "ldz", 32, 4300.0); landed(V("pin"), "ldp", 128, 4800.0)

    def C(k):
        return V("col", k, k + 1)
    P1, BC, BC16, INV2, P2 = [V("lu", a, b) for a, b in ((0, 16), (16, 24), (16, 32), (32, 48), (120, 136))]
    C33, C7, C1, C32, C0, QTR, M35 = [V("cst", a, b) for a, b in (
        (0, 128), (128, 256), (256, 384), (384, 512), (512, 640), (640, 896), (896, 912))]
    TAB = V("tab")
    iota(V("coli", 0, 1), [[0, 1]], 0, 1)
    iota(V("li", 0, 16), [[16, 8], [128, 2]])
    iota(V("li", 120, 136), [[2, 16]])
    iota(V("cidx"), [[1, 144]])
    iota(V("q2"), [[2, 8], [0, 16]])
    iota(V("li", 16, 32), [[0, 16]])
    iota(V("li", 32, 48), [[16, 2], [32, 8]])
    iota(V("base"), [[128, 16]])
    iota(V("blki"), [[16, 8], [0, 16]])

    ts(V("coli", 1, 2), V("coli", 0, 1), 15, Op.bitwise_and)
    ts(V("coli", 2, 3), V("coli", 0, 1), 7, Op.bitwise_and)
    ts(V("coli", 3, 4), V("coli", 0, 1), 8, Op.bitwise_and)
    cp(C(0), V("coli", 1, 2))
    ts(C(1), V("coli", 2, 3), 32.0, Op.mult)
    ts(P1, V("li", 0, 16), C(0), Op.add)
    ts(C(2), V("coli", 3, 4), 0.125, Op.mult, C(1), Op.add)
    cp(C(3), V("coli", 0, 1))
    ts(P2, V("li", 120, 136), C(2), Op.add)
    ts(C(4), C(3), C(0), Op.subtract)
    ts(ID(1.0), V("cidx", 0, 128), C(3), Op.is_equal)
    ts(C(5), C(4), 15.0, Op.add)
    ts(V("wp1"), V("cidx"), C(5), Op.is_equal)
    for x in IDS[1:]:
        act(ID(x), ID(1.0), Act.Identity, 0.0, x)
    for w, x in (("wn64", -64.0), ("wp64", 64.0), ("wn1", -1.0)):
        act(V(w), V("wp1"), Act.Identity, 0.0, x)
    for v, x in ((C33, 33.0), (C7, 7.0), (C1, 1.0), (C32, 32.0), (C0, 0.0), (M35, -3.5)):
        ms(v, x)
    cp(V("ta"), G(V("rin"), P1))
    tr(V("tb"), V("ta"))
    cp(S("ru", 0), G(V("tb"), P2))
    send("ru", S("ru", 0), 1)
    cp(S("rs", 0), S("ru", 0))
    cp(V("td"), G(V("pin"), P1))
    tr(V("te"), V("td"))
    cp(S("pp", 0, 0, 256), G(V("te"), P2))
    cp(S("jw", 0, 0, 128), V("q2"))
    ms(S("jw", 0, 128, 256), -1.0)
    act(C(6), C(0), Act.Identity, 0.0, 8.0)
    ts(V("lu", 16, 48), V("li", 16, 48), C(0), Op.add)
    ts(V("b16"), V("base"), C(6), Op.add)
    ts(V("blk"), V("blki"), C(4), Op.is_equal, -32.0, Op.mult)

    def LIM(k):
        return V("lim", k, k + 1)
    ts(LIM(0), V("thi", 0, 1), -1.0, Op.mult, -0.125, Op.add)
    act(LIM(1), LIM(0), Act.Copy)

    def sums(out, w, buf, src, rows, start, stop):
        def call():
            for a in range(16):
                last = g.tensor.matmul(ap(out), ap(V(w, 15 - a, 143 - a)), ap(V(buf, src + a, src + 256 * rows, 16)),
                                       start and a == 0, stop and a == 15)
            return last
        record("t", [out], [V(w), V(buf, src, src + 256 * rows)], call, lambda p: 16 * max(64, 16 * rows) * p["pe"])

    def rnames(t, row, k=1):
        c = 128 * (row // 8) + 16 * ((row + t) % 8)
        return S("ru", t, c, c + 16 * k)

    def ahead(t, kinds):
        for c in range(8):
            if kinds[c] in "ab":
                parts = [(0, 1), (1, 1)] if (2 * c + t) % 8 == 7 else [(0, 2)]
                for r, k in parts:
                    o, src = V("vv", 512 * c + 256 * r, 512 * c + 256 * (r + k)), G(TAB, rnames(t, 2 * c + r, k))
                    if kinds[c] == "a":
                        act(o, src, Act.Copy)
                    else:
                        cp(o, src)

    stage = [0]

    def sizes(kind, c, names, z, raw, dif, out):
        o = V(out, 512 * c, 512 * c + 512)
        if kind in "ab":
            bk = STAGE[stage[0] % len(STAGE)]
            stage[0] += 1
            mm(V(bk), ID(1.0), V(raw, 512 * c, 512 * c + 512), True, False)
            mm(V(bk, 0, 256), ID(-1.0), z, False, False)
            mm(V(bk, 256, 512), ID(-1.0), z, False, True)
            act(o, V(bk), Act.Abs)
            return
        for r in range(2):
            tt(V(dif, 512 * c + 256 * r, 512 * c + 256 * r + 256), G(TAB, names(2 * c + r)), z, Op.subtract)
        if kind == "v":
            ts(o, V(dif, 512 * c, 512 * c + 512), 0.0, Op.max, 2.0, Op.mult)
        else:
            act(o, V(dif, 512 * c, 512 * c + 512), Act.Abs)

    def quad(kinds, k, out, wabs, wdif, ab, dif, stop):
        vs = [c for c in (2 * k, 2 * k + 1) if kinds[c] == "v"]
        if vs:
            a = 32 * (vs[0] - 2 * k)
            sums(sub(out, a, a + 32 * len(vs)), wdif, dif, 512 * vs[0], 2 * len(vs), False, False)
        sums(out, wabs, ab, 1024 * k, 4, False, stop)

    KEYS = [V(bk, 0, 64) for bk in ("pb7", "pb6", "pkhi", "pklo")]
    X, WX = V("pklo", 128, 256), V("pklo", 256, 384)
    JP, FF = V("pkhi", 128, 256), V("pkhi", 256, 384)
    DP, PL, YS, UU = V("pb5", 0, 128), V("pb5", 128, 256), V("pb5", 256, 272), V("pb5", 272, 288)
    DLO, PS, EP, CNT = V("ps4", 0, 128), V("ps4", 128, 256), V("ps4", 256, 384), V("ps4", 384, 385)
    DR, AB, RF, S2 = [V("pb6", 128 * k, 128 * k + 128) for k in range(4)]
    DZ, AVG = V("pb7", 0, 256), V("pb7", 256, 512)

    def in_order(x, bks, tmp, out, dst, queues):
        open_ = len(set(bks)) == 4

        def add(k, j, start, stop):
            o, src, r = V(bks[k], 0, 256), V(x, 256 * j, 256 * j + 256), 64 >> k
            todo = [(1.0, 0, 256, 0)] if k == 3 else [(-1.0, 0, 256, 0)] + [
                (1.0, h + a, h + b, h + (a - r) % 128) for h in (0, 128) for a, b in ((0, r), (r, 128))]

            def call():
                for i, (f, a, b, c) in enumerate(todo):
                    res = g.tensor.matmul(ap(sub(o, a, b)), ap(ID(f)), ap(sub(src, c, c + b - a)), start and i == 0, stop and i == len(todo) - 1)
                return res
            record("t", [o], [ID(1.0), ID(-1.0), src], call, lambda p: sum(max(64, e[2] - e[1]) for e in todo) * p["pe"])
        for k in range(4):
            if open_:
                for k2 in range(k, 4):
                    add(k2, k, k == 0, k2 == k)
            else:
                for j in range(k + 1):
                    add(k, j, j == 0, j == k)
            if k < 3:
                tt(V(x, 256 * k + 256, 256 * k + 512), V("bits", 512 - 256 * k, 768 - 256 * k), V(bks[k], 0, 256), Op.mult)
        for b in range(8):
            tr(V(tmp, 32 * b, 32 * b + 32), V(bks[3], b, 256, 8))
        act(V(out), G(V(tmp), INV2), Act.Copy)
        for k, (sp_, sc_, rows) in enumerate(blocks()):
            store(queues[k % len(queues)], dst[rows, :], T[out][sp_, sc_], V(out))

    ahead(0, CFG["d0"])
    for t in range(ST):
        last = t == ST - 1
        seen.clear()
        seen["phase"] = "l" if last else "f" if t == 0 else ""
        kd, kf = CFG["d" if t else "d0"], CFG["flast" if last else "f"]
        z, J, W = S("zz", t), S("jw", t, 0, 128), S("jw", t, 128, 256)
        part = [S("pp", t, 128 * k, 128 * k + 128) for k in range(4)]
        plo, phi = (part[0::2], part[1::2]) if t else (part[:1], part[1:2])
        rlo, rhi = S("rs", t, 0, 128), S("rs", t, 128, 256)
        pf, c1, a1, e1 = [S("po", t, 128 * k, 128 * k + 128) for k in range(4)]
        J2, W2 = S("jo", t, 0, 128), S("jo", t, 128, 256)
        for k in CFG["quads"]:
            for c in (2 * k, 2 * k + 1):
                sizes(kd[c], c, lambda r: rnames(t, r), z, "vv", "dd", "ab")
        for i, k in enumerate(CFG["quads"]):
            key, a = KEYS[i], 64 * (k % 2)
            lin(key, [(1.0, sub(C33, 0, 64)), (-1.0, sub(J, a, a + 64)), (8.0 if k // 2 else -8.0, sub(W, a, a + 64))], True, False)
            quad(kd, k, key, "wn64", "wp64", "ab", "dd", True)
            if i == 0:
                act(V("khs", 0, 64), key, Act.Copy)
                key = V("khs", 0, 64)
            else:
                tt(V("m1", 64 * i - 64, 64 * i), key, V("m1", 64 * i - 128, 64 * i - 64) if i > 1 else V("khs", 0, 64), Op.max)
            act(V("fl", 64 * k, 64 * k + 64), key, Act.Sign, LIM(1), -1.0 / 64)
        if t + 2 < ST:
            send("ru", S("ru", t + 1), t + 2, [V("m1", 64, 128)])
        if not last:
            send("rs", S("rs", t), t + 1, [V("m1", 64, 128)])
        tt(V("m1", 192, 224), V("m1", 128, 160), V("m1", 160, 192), Op.max)
        tt(V("mi", 0, 16), V("m1", 192, 208), V("m1", 208, 224), Op.max)
        ts(V("mi", 16, 32), V("mi", 0, 16), 63, Op.bitwise_and)
        tt(V("un"), G(V("mi", 16, 32), BC), J, Op.add)
        ts(V("sp"), V("un"), M16, Op.add, M16 + 32, Op.is_equal)
        ts(V("rr"), V("un"), M16, Op.add, M16, Op.subtract)
        lin(DP, [(1.0, v) for v in phi] + [(-1.0, v) for v in plo])
        lin(PL, [(1.0, v) for v in plo])
        tt(V("t3"), V("sp"), DP, Op.mult)
        tt(pf, V("t3"), PL, Op.add)
        cp(V("pu"), pf)
        lin(DLO, [(1.0, v) for v in phi] + [(-1.0, v) for v in plo] + [(-2.0, V("t3"))])
        lin(PS, [(1.0, v) for v in phi] + [(-1.0, V("t3"))])
        if not last:
            send("pa", pf, t + 1)
        lin(JP, [(1024.0, C7), (1024.0, V("un")), (-1024.0, V("rr"))])
        tt(V("mx"), pf, JP, Op.max)
        act(J2, JP, Act.Identity, 0.0, 1.0 / 1024)
        if last:
            cp(V("jp", 0, 16), sub(JP, 0, 16))
            for k in range(3):
                ts(V("jp", 16 * k + 16, 16 * k + 32), V("jp", 0, 16), 11 + k, Op.arith_shift_right, 1, Op.bitwise_and)
            cp(V("tc", 0, 48), V("jp", 16, 64))
            for k in range(3):
                act(V("bits", 256 * k, 256 * k + 256), G(V("tc", 16 * k, 16 * k + 16), BC16), Act.Copy)

        def ysum():
            for q in range(8):
                r = g.tensor.matmul(ap(YS), ap(ID(1.0)), ap(V("mx", 16 * q, 16 * q + 16)), q == 0, q == 7)
            return r
        record("t", [YS], [ID(1.0), V("mx")], ysum, lambda p: 512 * p["pe"])
        ts(V("yu"), YS, -28.0 * 2048, Op.add)
        for c in range(4):
            if kf[c] in "ab":
                (cp if kf[c] == "b" else lambda o, a: act(o, a, Act.Copy))(
                    V("vp", 512 * c, 512 * c + 512), G(TAB, V("pu", 32 * c, 32 * c + 32)))
        if CFG["y"] == "v":
            cp(V("yy"), G(TAB, V("yu")))
            lin(DZ, [(1.0, V("yy")), (-1.0, z)])
            act(S("zo", t), DZ, Act.Abs)
        else:
            tt(V("dz"), G(TAB, V("yu")), z, Op.subtract)
            act(V("yy"), G(TAB, V("yu")), Act.Copy)
            act(S("zo", t), V("dz"), Act.Abs)
        if not last:
            send("zz", S("zo", t), t + 1)
        else:
            store("s", T.yz[:], ap(S("zo", t)), S("zo", t))
        lin(UU, [(1.0, M35)], True, False)
        sums(UU, "wp1", "yy", 0, 1, False, True)
        ts(V("r8", 0, 16), UU, M8, Op.add, M8, Op.subtract)
        tt(V("r8", 16, 32), UU, V("r8", 0, 16), Op.subtract)
        lin(UU, [(1.0, V("r8", 16, 32)), (1.0, V("b16"))])
        ts(V("uu"), UU, 3.5, Op.add)
        lin(AVG, [(1.0, V("yy")), (1.0, z)])
        ts(V("avg"), AVG, 0.5 - 2.0 ** -11, Op.mult)
        lin(X, [(1.0, V("un"), 16), (-8.0, W, 16)])
        act(V("ww"), X, Act.Abs, -26.0)
        ts(V("sr"), V("ww"), M16, Op.add, M16 + 16, Op.is_equal)
        turn = 16 * (t + 1)
        lin(DR, [(1.0, rhi, turn), (-1.0, rlo, turn)])
        lin(AB, [(1.0, V("fl", 0, 128), 16), (1.0, V("fl", 128, 256), 16)])
        tt(V("t2"), V("sr"), DR, Op.mult)
        tt(V("s1"), V("sr"), AB, Op.mult)
        lin(RF, [(1.0, C32), (1.0, rlo, turn), (1.0, V("t2"))])
        lin(S2, [(1.0, C1), (1.0, V("fl", 0, 128), 16), (-2.0, V("sr")), (-1.0, V("s1"))])
        tt(V("s3"), J2, S2, Op.mult)
        lin(WX, [(1.0, V("s3")), (1.0, V("sr"))])
        act(W2, WX, Act.Sign, -0.5)
        if not last:
            send("jw", S("jo", t), t + 1)
        if t:
            tt(V("prod"), pf, RF, Op.mult)
            ts(V("pa"), V("prod"), LIM(2), Op.add)
        else:
            tt(V("pa"), pf, RF, Op.mult)
        ts(V("new"), V("pa"), 5, Op.arith_shift_right, 2047, Op.bitwise_and)
        if last:
            tt(V("t2"), W2, DR, Op.mult)
            for h in range(2):
                lin(V("pklo", 128 * h, 128 * h + 128), [(-0.5 if h else 0.5, V("t2")), (0.5, rlo, turn), (0.5, rhi, turn)])
            cp(V("xr", 0, 256), V("pklo", 0, 256))
            in_order("xr", ("pb6", "pklo", "pb6", "pklo"), "ta", "orr", T.yr, "s")
        for c in range(4):
            sizes(kf[c], c, lambda r: V("pu", 16 * r, 16 * r + 16), V("yy"), "vp", "dp", "abp")
        cp(G(TAB, V("uu")), V("avg"))
        if last:
            store("s", T.yx[:], ap(TAB), TAB, 5000.0)
        else:
            ahead(t + 1, CFG["d"])
        lin(FF, [(1.0, C0)], True, False)
        for k in range(2):
            quad(kf, k, sub(FF, 64 * k, 64 * k + 64), "wp1", "wn1", "abp", "dp", k == 1)
        if CFG["e"] == "v":
            ts(V("ee"), FF, LIM(1), Op.add, 0.0, Op.is_gt)
        else:
            act(V("sg"), FF, Act.Sign, LIM(1))
            act(V("ee"), V("sg"), Act.Relu)
        act(V("eb"), V("ee"), Act.Identity, 1.0, -1.0, None if last else V("cnt", 0, 1))
        lin(EP, [(1.0, V("ee"))])
        if last:
            tt(V("pb7", 0, 128), V("ee"), DLO, Op.mult)
            tt(c1, V("eb"), PS, Op.mult)
            tt(V("pb7", 128, 256), V("new"), EP, Op.mult)
            tt(V("xp", 0, 128), pf, V("pb7", 0, 128), Op.add)
            tt(V("xp", 128, 256), c1, V("pb7", 128, 256), Op.add)
        else:
            tt(a1, V("ee"), DLO, Op.mult)
            tt(c1, V("eb"), PS, Op.mult)
            tt(e1, V("new"), EP, Op.mult)
            send("pb", S("po", t, 128, 512), t + 1)
            mm(CNT, V("blk"), V("cnt", 0, 1), True, True)
            act(LIM(2), CNT, Act.Copy)
            cp(V("ai", 0, 1), LIM(2))
            ts(V("ai", 1, 2), V("ai", 0, 1), 5, Op.arith_shift_right, 31, Op.bitwise_and)
            ts(LIM(1), V("ai", 1, 2), -1.0, Op.mult, LIM(0), Op.add)

    seen.clear()
    seen["phase"] = "z"
    in_order("xp", ("ps0", "ps2", "pb6", "pklo"), "tb", "op", T.yp, "sa")
    emit()
    g.sync.wait_ge(T.sem.sto, cnt["sto"])
    for s in ("sent", "cv", "ca", "ct", "cg"):
        g.wait_ge(T.sem[s], cnt[s])
